import numpy as np, ml_dtypes
CORES = [13,21,141,149]
N = 4
BF = ml_dtypes.bfloat16
def gentries(a):
    return np.ascontiguousarray(a.reshape(8, 16, -1).transpose(0, 2, 1)).reshape(8, -1)
def gtable(e):
    e = np.asarray(e); return np.ascontiguousarray(e.reshape(8, -1, 16).transpose(0, 2, 1)).reshape(128, -1).astype(np.int32)
W, E, P = 1280, 448, 5
M = (P - 1) // 2
def lens(rng, n, rw, how):
    i = np.arange(n)
    if how == 0: v = i % (P + 1)
    elif how == 1: v = np.where(i < (W - n - rw * (2 + M)) // ((P + 1) // 2), P, 0)
    elif how == 2: v = np.where(i % 10 < 9, 0, 1 + (i // 10) % P)
    elif how == 3: v = i % 3
    else: v = np.full(n, 1)
    return rng.permutation(v)
def colours(rng, ln, lo, hi):
    n = len(ln); a = rng.integers(lo, hi, n); b = lo + (a - lo + rng.integers(1, hi - lo, n)) % (hi - lo)
    x, y = np.maximum(a, b), np.minimum(a, b); z = ln == 0; same = rng.random(n) < 0.5
    return np.where(z, x, a), np.where(z, np.where(same, x, y), b)
def special(rng, rw):
    kd = (np.arange(rw) + rng.integers(0, 7)) % 7; q = rng.random(rw) < 0.5
    s = np.sort(np.argsort(rng.random((rw, 16)), axis=1)[:, :3], axis=1); j = rng.integers(0, 3, rw)
    j = np.where(kd == 0, 2, np.where((kd == 1) | (kd == 5), j % 2, j))
    s = np.take_along_axis(s, np.array([[2, 0, 1], [1, 0, 2], [0, 1, 2]])[j], axis=1)
    add, mul, span = np.array([[2, 2, 1, 1, 3, 0, 2], [2, 1, 2, 1, 1, 1, 1], [M, 1, 2, 4, 2, 1, 3]])[:, kd]
    return kd, q, s[:, 0], s[:, 1], s[:, 2], add + mul * (span * rng.random(rw)).astype(np.int64)
def way(v, ln, pl, pr):
    X = np.full((len(ln), P + 1), -1); X[:, 0] = v
    for i in range(1, P + 1):
        m = ln >= i; n = int(np.count_nonzero(m))
        if i % 2: X[m, i] = pl[:n]; pl = pl[n:]
        else: X[m, i] = pr[:n]; pr = pr[n:]
    return X, pl, pr
def plant(LT, RT, X, ln, a, b):
    for i in range(1, P + 1):
        m = ln >= i; p, x = X[m, i - 1], X[m, i]
        if i % 2: c = a[m]; RT[c, p] = x; LT[c, x] = p
        else: c = b[m]; LT[c, p] = x; RT[c, x] = p
    e = X[np.arange(len(ln)), ln]; m = ln % 2 == 0
    RT[a[m], e[m]] = -1; LT[b[~m], e[~m]] = -1
def graph(rng, rw, H, how, drop, order):
    LT = np.full((16, W), -2); RT = np.full((16, W), -2); LM = np.zeros((16, W), bool); RM = np.zeros((16, W), bool)
    C = np.arange(16)[:, None]; F = E - rw; S = E // 8
    if order == 0: nl, nr = rng.permutation(W), rng.permutation(W)
    elif order == 1: nl, nr = np.arange(W), np.arange(W)
    else: nl, nr = np.arange(W)[::-1], np.arange(W)[::-1]
    kd, q, a0, b0, e, l0 = special(rng, rw)
    ln = np.concatenate([l0, lens(rng, F, rw, how)])
    a, b = colours(rng, ln, 0, H); a[:rw] = a0; b[:rw] = b0
    u, v = nl[:E], nr[:E]; X, zl, zr = way(v, ln, nl[E:], nr[E:])
    plant(LT, RT, X, ln, a, b)
    LT[a, u] = -1; RT[b, v] = -1; LM[:, u] = C < a; RM[:, v] = C < b
    u0, v0, Z = u[:rw], v[:rw], X[:rw]; end = Z[np.arange(rw), l0]
    ua, zl = zl[:rw], zl[rw:]; zz, zr = zr[:rw], zr[rw:]
    m = (kd == 5) & q; n = int(np.count_nonzero(m)); p = np.array(ua); p[m] = zl[:n]; zl = zl[n:]
    c = np.where((kd == 3) | ((kd == 4) & q), b0, np.where(m | (kd == 6), e, a0))
    d = np.where((kd >= 2) & (kd <= 4), e, np.where((kd == 6) & q, a0, b0))
    y = np.where(kd < 2, end, np.where(kd == 4, Z[:, 2], np.where(kd == 6, zz, v0))); u1 = np.where(kd == 2, end, ua)
    s = np.where(kd == 3, Z[:, 1], np.where(kd == 4, np.where(q, Z[:, 3], Z[:, 1]), np.where(m, p, u0)))
    LM[:, u1] = C < c; RM[:, y] = C < d
    i = kd != 2; LT[c[i], ua[i]] = -1
    i = kd > 1; RT[d[i], y[i]] = -1
    i = (kd > 0) & (kd < 6); LT[d[i], s[i]] = zz[i]; RT[d[i], zz[i]] = s[i]; RT[c[i], zz[i]] = -1
    RT[e[m], v0[m]] = p[m]; LT[e[m], p[m]] = v0[m]
    i = kd == 6; x = Z[i, 1]; RT[e[i], zz[i]] = x; LT[e[i], x] = zz[i]; RT[e[i], np.where(q, Z[:, 2], v0)[i]] = -1
    i = kd == 0; LT[b0[i], u0[i]] = -1
    pu = rng.permutation(np.concatenate([u[rw:], zl[:S]])); pv = rng.permutation(np.concatenate([v[rw:], zr[:S]]))
    u2, v2 = pu[:F], pv[:F]; tl, tr = X[rw:, 1::2], X[rw:, 2::2]
    restl = rng.permutation(np.concatenate([pu[F:], zl[S:], tl[tl >= 0]])); restr = rng.permutation(np.concatenate([pv[F:], zr[S:], tr[tr >= 0]]))
    still = np.zeros(W, bool); still[v[(ln == 0) & (a > b)]] = True; z = still[v2]; g = ~z
    l2 = lens(rng, F, rw, how); l2[z] = 0
    c, d = colours(rng, l2, H, 16); Y, _, _ = way(v2, l2, restl, restr)
    plant(LT, RT, Y, l2, c, d)
    LT[c, u2] = -1; LM[:, u2] = LM[:, u2] | (C < c)
    RT[d[g], v2[g]] = -1; RM[:, v2[g]] = RM[:, v2[g]] | (C < d[g])
    for k in range(16):
        x, w = np.flatnonzero(LT[k] == -2), np.flatnonzero(RT[k] == -2); n = min(len(x), len(w))
        x = x[np.argsort(rng.random(len(x)) - 2.0 * LM[k, x])][:n]; w = rng.permutation(w[np.argsort(rng.random(len(w)) - 2.0 * RM[k, w])][:n])
        keep = LM[k, x] | RM[k, w] | (rng.random(n) >= drop); x, w = x[keep], w[keep]
        LT[k, x] = w; RT[k, w] = x
    k1 = rng.permutation(E) if order == 0 else np.arange(E); k2 = rng.permutation(E)
    return np.where(LT < 0, W, LT), np.where(RT < 0, W, RT), np.stack([u[k1], np.concatenate([u1, u2])[k2]]), np.stack([v[k1], np.concatenate([y, v2])[k2]])
def make(rng, pick):
    lt = np.zeros((N, 128, W), np.int32); rt = np.zeros((N, 128, W), np.int32); eu = np.zeros((N, 8, 2, E), np.int64); ev = np.zeros((N, 8, 2, E), np.int64)
    for q in range(N):
        for g in range(8):
            s = slice(16 * g, 16 * g + 16)
            lt[q, s], rt[(q + 1) % N, s], eu[q, g], ev[q, g] = graph(rng, *pick(q, g))
    return {"lt": lt, "rt": rt, "eu": np.stack([gtable(x.reshape(8, -1)) for x in eu]), "ev": np.stack([gtable(x.reshape(8, -1)) for x in ev])}
def setup_inputs(rng):
    return make(rng, lambda q, g: (E // 8, int(rng.integers(6, 11)), 0, 0.3 * rng.random(), 0))
def setup_inputs_again(rng):
    return make(rng, lambda q, g: (E // 4, int(rng.integers(6, 11)), 3, 0.3 * rng.random(), 0))
def setup_inputs_long(rng):
    return make(rng, lambda q, g: (0 if (q + g) % 4 == 3 else E // 8, int(rng.integers(6, 11)), 4 if (q + g) % 4 == 3 else 1, 0.3 * rng.random(), 0))
def setup_inputs_order(rng):
    return make(rng, lambda q, g: (E // 8, int(rng.integers(6, 11)), 0, 1.0 if g % 4 < 2 else 0.5, 1 + g % 2))
def setup_inputs_short(rng):
    return make(rng, lambda q, g: (E // 8, int(rng.integers(6, 11)), 2, 0.3 * rng.random(), 0))
def setup_inputs_spread(rng):
    return make(rng, lambda q, g: (int(rng.choice(np.array([1, E // 8]))), int(rng.integers(4, 13)), int(rng.integers(0, 4)), rng.random(), 0))
def load_all(lt, rt, eu, ev):
    none = np.full((8 * N, 16, 1), W, np.int64)
    L = np.concatenate([lt.astype(np.int64).reshape(8 * N, 16, W), none], axis=2)
    R = np.concatenate([np.roll(rt, -1, axis=0).astype(np.int64).reshape(8 * N, 16, W), none], axis=2)
    U, V = [np.stack([gentries(x) for x in t]).astype(np.int64).reshape(8 * N, 2, E) for t in (eu, ev)]
    return L, R, U, V
def turn(L, R, u, v):
    k = np.arange(8 * N)[:, None]
    fu = L[k, :, u] == W; fv = R[k, :, v] == W
    a = np.argmax(fu, axis=2); b = np.argmax(fv, axis=2); free = bool(np.all(np.any(fu, axis=2)) and np.all(np.any(fv, axis=2)))
    xs = [v]
    for i in range(P + 1):
        T = R if i % 2 == 0 else L; x = xs[-1]
        p, q = T[k, a, x], T[k, b, x]
        xs.append(p if i % 2 == 0 else q)
        T[k, a, x] = q; T[k, b, x] = p
    L[k, a, u] = v; R[k, a, v] = u
    return a, free, xs
def check_inputs(d):
    bad = []
    for k, hi in (("lt", W), ("rt", W), ("eu", W - 1), ("ev", W - 1)):
        if np.min(d[k]) < 0 or np.max(d[k]) > hi: bad.append("range of " + k)
    if bad: return bad
    L, R, U, V = load_all(d["lt"], d["rt"], d["eu"], d["ev"]); own = np.arange(W + 1)
    for A, B in ((L, R), (R, L)):
        if np.any((A < W) & (np.take_along_axis(B, A, 2) != own)): bad.append("lt and rt tell the same edges")
    if bad: return bad
    for t in range(2):
        a, free, xs = turn(L, R, U[:, t], V[:, t])
        if not free: bad.append("a free colour at both ends")
        if np.any(xs[P + 1] < W): bad.append("paths of at most P edges")
        for side in ([U[:, t]] + xs[1:P + 1:2], xs[0:P + 1:2]):
            s = np.sort(np.concatenate(side, axis=1), axis=1)
            if np.any((s[:, 1:] == s[:, :-1]) & (s[:, 1:] < W)): bad.append("different vertices in a round")
        if bad: return bad
    return bad
def reference(lt, rt, eu, ev):
    L, R, U, V = load_all(lt, rt, eu, ev); got = []
    for t in range(2):
        a, free, xs = turn(L, R, U[:, t], V[:, t]); got.append(a)
    return {"yl": np.ascontiguousarray(L[:, :, :W]).reshape(N, 128, W).astype(np.float32), "ya": np.concatenate(got, axis=1).reshape(N, 8, 2 * E).astype(np.float32)}

@@ -1,0 +1,397 @@
+from concourse.bass import DstId, RemoteDMATransfer
+from concourse.mybir import AluOpType as ALU, ActivationFunctionType as ACT
+
+W, E, K = 1280, 448, 28
+SH = 32
+NL, NR = W + SH, W
+LW, RW = 1768, 1736
+BIG = 2048.0
+CH = W // 4
+WORLD = 256
+
+SCRATCH = {
+    "rti": ("sbuf", [128, W], "int32"), "rtu": ("sbuf", [128, W], "float16"),
+    "hop": ("sbuf", [128, CH], "float16"), "land": ("sbuf", [128, W], "float16"),
+    "lti": ("sbuf", [128, NL], "int32"), "Lw": ("sbuf", [128, LW], "float32"),
+    "Rr": ("sbuf", [128, W + 8], "float32"), "Rw": ("sbuf", [128, RW], "float32"),
+    "eui": ("sbuf", [128, 2 * K], "int32"), "evi": ("sbuf", [128, 2 * K], "int32"),
+    "uo": ("sbuf", [128, 2 * K], "uint16"), "vo": ("sbuf", [128, 2 * K], "uint16"),
+    "iw": ("sbuf", [128, NL], "float32"),
+    "nv": ("sbuf", [128, 2 * E], "float16"), "nu": ("sbuf", [128, E], "float16"),
+    "xo": ("sbuf", [128, 6 * K], "uint16"), "so": ("sbuf", [128, 6 * K], "uint16"),
+    "tt": ("sbuf", [128, 6 * K], "float32"), "mx": ("sbuf", [128, 6 * K], "float32"),
+    "Gu": ("sbuf", [128, E], "float32"), "Xu": ("sbuf", [128, E], "float32"), "Zu": ("sbuf", [128, E], "float32"),
+    "fu": ("sbuf", [128, E], "bfloat16"), "sv": ("sbuf", [128, E], "bfloat16"),
+    "yas": ("sbuf", [128, 2 * E], "float32"),
+    "ones": ("sbuf", [128, 128], "float32"), "Oa": ("sbuf", [128, 128], "float32"), "O32": ("sbuf", [128, 128], "float32"),
+    "I32": ("sbuf", [128, 128], "float32"), "T32": ("sbuf", [128, 128], "float32"), "nI32": ("sbuf", [128, 128], "float32"),
+    "O16": ("sbuf", [128, 128], "float16"), "nO16": ("sbuf", [128, 128], "float16"), "I16": ("sbuf", [128, 128], "float16"),
+    "B16": ("sbuf", [128, 144], "float16"), "KE": ("sbuf", [128, K], "float16"), "kf": ("sbuf", [128, K], "float32"),
+    "KL": ("sbuf", [128, E], "float16"), "KR": ("sbuf", [128, E], "float16"),
+    "Mb": ("sbuf", [128, 128], "bfloat16"), "IB": ("sbuf", [128, 128], "bfloat16"), "I2b": ("sbuf", [128, 128], "bfloat16"),
+    "nIb": ("sbuf", [128, 128], "bfloat16"), "Yw": ("sbuf", [128, 8], "bfloat16"),
+    "pi": ("sbuf", [128, 1], "int32"), "ci": ("sbuf", [128, 1], "int32"), "cf": ("sbuf", [128, 1], "float32"),
+    "bL": ("sbuf", [128, 1], "float32"), "bR": ("sbuf", [128, 1], "float32"), "bM": ("sbuf", [128, 1], "float32"),
+    "nn": ("sbuf", [128, 8], "float32"),
+}
+for _i in range(5):
+    SCRATCH["H%d" % _i] = ("sbuf", [128, E], "float16")
+for _i in range(6):
+    SCRATCH["G%d" % _i] = ("sbuf", [128, E], "float32")
+    SCRATCH["E%d" % _i] = ("sbuf", [128, E], "float32")
+for _t in range(2):
+    for _n in ("ma", "mb", "sg"):
+        SCRATCH["%s%d" % (_n, _t)] = ("sbuf", [128, E], "bfloat16")
+for _n in ("PX0", "PX1", "PX2", "PD0", "PD1", "PM0", "PM1", "PM2"):
+    SCRATCH[_n] = ("psum", [128, 512], "float32")
+
+SEMAPHORES = ["sV", "sA", "sP", "sG", "hopin", "sent", "arr0", "arr1", "arr2", "arr3",
+              "dR0", "dR1", "dL", "dU", "dV", "dC", "dY0", "dY1", "dO"]
+
+
+def routes(T, topo):
+    out = []
+    n = len(T.cores)
+    for q in range(n):
+        s, d = T.cores[q], T.cores[(q - 1) % n]
+        far, near = {}, {}
+        for c in range(WORLD):
+            if T.rank_of(c) is None and topo.mates(c, d) and topo.may_write(s, c) and topo.may_write(c, d):
+                far.setdefault(topo.die(c), c)
+        for c in topo.cores_of(s):
+            if T.rank_of(c) is None and topo.may_write(c, d):
+                near.setdefault(topo.die(c), c)
+        far, near = [far[k] for k in sorted(far)], [near[k] for k in sorted(near)]
+        off = topo.engines(s, far[0])
+        on = [e for e in topo.engines(s, near[0]) if e not in off]
+        for k, (c, eng) in enumerate(((far[0], off[:len(off) // 2]), (far[1], off[len(off) // 2:]),
+                                      (near[0], on[:len(on) // 2]), (near[1], on[len(on) // 2:]))):
+            out.append((s, c, d, k, eng))
+    return out
+
+
+def bits(engines):
+    return sum(1 << e for e in engines)
+
+
+def rank_program(g, core, T, topo):
+    rts = routes(T, topo)
+    if T.rank_of(core) is None:
+        for s, c, d, k, eng in rts:
+            if c == core:
+                rid, pid = topo.addr(d, core)
+                g.wait_ge(T.sem.hopin, len(eng))
+                g.remote_dma(T.land[:, k * CH:(k + 1) * CH], T.hop[:], T.sem["arr%d" % k], T.sem.sent, pid, rid,
+                             topo.mask(core, d))
+                g.wait_ge(T.sem.sent, len(topo.engines(core, d)))
+        return
+
+    Q = {"V": g.vector, "A": g.scalar, "P": g.tensor, "G": g, "S": g.sync}
+    own = {"V": "sV", "A": "sA", "P": "sP", "G": "sG"}
+    known = {e: {} for e in Q}
+    count, clock, writer, readers = {}, {}, {}, {}
+
+    def wait(e, evs):
+        need = {}
+        for s, v in evs:
+            if not (e == "P" and s == "sP") and known[e].get(s, 0) < v:
+                need[s] = max(need.get(s, 0), v)
+        for s in sorted(need, key=lambda x: x == own.get(e)):
+            v = need[s]
+            if known[e].get(s, 0) < v:
+                Q[e].wait_ge(T.sem[s], v)
+                for s2, v2 in clock.get((s, v), {s: v}).items():
+                    known[e][s2] = max(known[e].get(s2, 0), v2)
+
+    def deps(rd, wr):
+        evs = [writer[k] for k in rd if k in writer]
+        for k in wr:
+            evs += readers.get(k, [])
+            if k in writer:
+                evs.append(writer[k])
+        return evs
+
+    def done(e, ins, rd, wr, sem, n):
+        count[sem] = count.get(sem, 0) + n
+        ins.then_inc(T.sem[sem], n)
+        ev = (sem, count[sem])
+        clock[ev] = dict(known[e])
+        clock[ev][sem] = count[sem]
+        for k in rd:
+            readers.setdefault(k, []).append(ev)
+        for k in wr:
+            writer[k] = ev
+            readers[k] = []
+
+    def op(e, fn, rd, wr):
+        wr = wr + [k for k in rd if k[0] == "P"]
+        wait(e, deps(rd, wr))
+        done(e, fn(), rd, wr, own[e], 1)
+
+    def dma(e, sem, out, in_, rd, wr):
+        wait(e, deps(rd, wr))
+        done(e, Q[e].dma_start(out, in_), rd, wr, sem, 16)
+
+    def mm(bank, out, terms, start=True, stop=True):
+        rd = []
+        for j, (lhsT, rhs, keys) in enumerate(terms):
+            wait("P", deps(keys, [bank]))
+            ins = g.tensor.matmul(out, lhsT, rhs, start and j == 0, stop and j == len(terms) - 1)
+            rd += keys
+        done("P", ins, rd, [bank], "sP", 1)
+
+    V, A = g.vector, g.scalar
+
+    def ts(out, in0, s1, s2, op0, op1, rd, wr):
+        if s2 is None:
+            op("V", lambda: V.tensor_scalar(out, in0, s1, None, op0), rd, wr)
+        else:
+            op("V", lambda: V.tensor_scalar(out, in0, s1, s2, op0, op1), rd, wr)
+
+    def tt(out, in0, in1, alu, rd, wr):
+        op("V", lambda: V.tensor_tensor(out, in0, in1, alu), rd, wr)
+
+    def cp(out, in_, rd, wr):
+        op("V", lambda: V.tensor_copy(out, in_), rd, wr)
+
+    def fill(ap, val, key):
+        op("V", lambda: V.memset(ap, val), [], [key])
+
+    def act(out, in_, func, rd, wr, bias=0.0, scale=1.0):
+        op("A", lambda: A.activation(out, in_, func, bias=bias, scale=scale), rd, wr)
+
+    def col(buf, i, a=0, b=K):
+        return T[buf][:, i * K + a:i * K + b]
+
+    def full(name, a=0, b=K):
+        return T[name][:, 16 * a:16 * b]
+
+    h = W // 2
+    dma("S", "dR0", T.rti[:, 0:h], T.rt[:, 0:h], [], ["rti0"])
+    dma("S", "dR1", T.rti[:, h:W], T.rt[:, h:W], [], ["rti1"])
+    dma("S", "dL", T.lti[:, SH:NL], T.lt[:], [], ["lti"])
+    dma("A", "dU", T.eui[:], T.eu[:], [], ["eui"])
+    dma("A", "dV", T.evi[:], T.ev[:], [], ["evi"])
+
+    fill(T.ones[:], 1.0, "ones")
+    fill(T.nn[:], float(NL), "nn")
+    op("G", lambda: g.iota(T.pi[:], [[0, 1]], 0, 1), [], ["pi"])
+    op("G", lambda: g.iota(T.kf[:], [[1, K]], 0, 0, allow_small_or_imprecise_dtypes=True), [], ["kf"])
+    op("G", lambda: g.affine_select(T.Oa[:], T.ones[:], [[-16, 8], [0, 16]], ALU.is_ge, 0.0, 0, 1), ["ones"], ["Oa"])
+    op("G", lambda: g.affine_select(T.I32[:], T.ones[:], [[-1, 128]], ALU.is_equal, 0.0, 0, 1), ["ones"], ["I32"])
+    op("G", lambda: g.affine_select(T.O32[:], T.Oa[:], [[16, 8], [0, 16]], ALU.is_ge, 0.0, 15, -1), ["Oa"], ["O32"])
+    q4 = NL // 4
+    op("G", lambda: g.iota(T.iw[:, 0:q4], [[-1, q4]], 0, 0, allow_small_or_imprecise_dtypes=True), [], ["iw0"])
+    op("G", lambda: g.affine_select(T.T32[:], T.O32[:], [[1, 128]], ALU.is_gt, 0.0, 0, -1), ["O32"], ["T32"])
+    act(T.Rr[:, W:W + 8], T.nn[:], ACT.Silu, ["nn"], ["Rrn"])
+    fill(T.B16[:], 0.0, "B16")
+    fill(T.KL[:], W / 16.0, "KL")
+    fill(T.KR[:], NL / 16.0, "KR")
+    fill(T.lti[:, 0:SH], 0, "lti0")
+    fill(T.Lw[:, 0:SH], 0.0, "Lw0")
+    fill(T.Lw[:, NL:NL + 8], float(NR), "Lwn")
+    ts(T.ci[:], T.pi[:], 15, None, ALU.bitwise_and, None, ["pi"], ["ci"])
+    ts(T.KE[:], T.kf[:], 1.0 / 1024, None, ALU.mult, None, ["kf"], ["KE"])
+    cp(T.cf[:], T.ci[:], ["ci"], ["cf"])
+    cp(T.I16[:], T.I32[:], ["I32"], ["I16"])
+    ts(T.bL[:], T.cf[:], float(K), float(NL + 1 - 1024 * NL), ALU.mult, ALU.add, ["cf"], ["bL"])
+    ts(T.bR[:], T.cf[:], float(K), float(NR + 1 - 1024 * NR), ALU.mult, ALU.add, ["cf"], ["bR"])
+    ts(T.bM[:], T.cf[:], -0.5, 0.5, ALU.mult, ALU.add, ["cf"], ["bM"])
+    ts(T.uo[:], T.eui[:], float(SH), None, ALU.add, None, ["eui"], ["uo"])
+    cp(T.vo[:], T.evi[:], ["evi"], ["vo"])
+    cp(T.O16[:], T.O32[:], ["O32"], ["O16"])
+    ts(T.nO16[:], T.O32[:], -1.0, None, ALU.mult, None, ["O32"], ["nO16"])
+    cp(T.B16[:, 15:143:16], T.O32[:, 0:128:16], ["O32", "B16"], ["B16"])
+    act(T.IB[:], T.I32[:], ACT.Identity, ["I32"], ["IB"], scale=BIG)
+    act(T.nI32[:], T.I32[:], ACT.Identity, ["I32"], ["nI32"], scale=-1.0)
+    act(T.iw[:, q4:2 * q4], T.iw[:, 0:q4], ACT.Identity, ["iw0"], ["iw1"], bias=-float(q4))
+    act(T.iw[:, 2 * q4:3 * q4], T.iw[:, 0:q4], ACT.Identity, ["iw0"], ["iw2"], bias=-float(2 * q4))
+    act(T.iw[:, 3 * q4:NL], T.iw[:, 0:q4], ACT.Identity, ["iw0"], ["iw3"], bias=-float(3 * q4))
+    act(T.I2b[:], T.I32[:], ACT.Identity, ["I32"], ["I2b"], scale=2.0)
+    act(T.nIb[:], T.I32[:], ACT.Identity, ["I32"], ["nIb"], scale=-1.0)
+    act(T.Yw[:], T.O32[:, 0:128:16], ACT.Identity, ["O32", "cf"], ["Yw"], scale=T.cf[:])
+    IW = ["iw0", "iw1", "iw2", "iw3"]
+
+    mine = [r for r in rts if r[0] == core]
+    for half in range(2):
+        cp(T.rtu[:, half * h:(half + 1) * h], T.rti[:, half * h:(half + 1) * h], ["rti%d" % half], ["rtu%d" % half])
+        wait("G", [writer["rtu%d" % half]])
+        trs = []
+        for s, c, d, k, eng in mine[2 * half:2 * half + 2]:
+            rid, pid = topo.addr(c, core)
+            trs.append(RemoteDMATransfer(dst_ids=[DstId(rid=rid, pnc=pid)], dma_engine_mask=bits(eng), remote_sem=T.sem.hopin,
+                                         src=T.rtu[:, k * CH:(k + 1) * CH], dst=T.hop[:]))
+            count["sent"] = count.get("sent", 0) + len(eng)
+        g.remote_dma_fused(trs, local_sem=T.sem.sent)
+    tt(T.Mb[:], T.I32[:], T.T32[:], ALU.subtract, ["I32", "T32"], ["Mb"])
+
+    Lg, Ls = T.Lw[:, 0:NL + 8], T.Lw[:]
+    px = [0]
+
+    def u_terms(t):
+        return [(T.I16[:], T.nv[:, t * E:(t + 1) * E], ["I16", "nv%d" % t]), (T.IB[:], full("ma%d" % t), ["IB", "ma%d" % t])]
+
+    def first_free(bank, flags):
+        mm(bank, full(bank), [(T.Mb[:], full(flags), ["Mb", flags])])
+
+    def colours_out(t, bank):
+        mm(bank, T[bank][0:8, 0:E], [(T.Yw[:], full("ma%d" % t), ["Yw", "ma%d" % t])])
+
+    def colours_store(t, bank):
+        act(T.yas[0:8, t * E:(t + 1) * E], T[bank][0:8, 0:E], ACT.Copy, [bank], ["yas%d" % t])
+        dma("S", "dY%d" % t, T.ya[:, t * E:(t + 1) * E], T.yas[0:8, t * E:(t + 1) * E], ["yas%d" % t], [])
+
+    def scatter_u(t, a=0, b=K):
+        tt(Ls.indirect(col("uo", t, a, b)), full("Gu", a, b), full("Xu", a, b), ALU.subtract, ["uo", "Gu", "Xu"], ["L"])
+
+    cp(T.nv[:, 0:E], T.iw[:].indirect(col("vo", 0)), IW + ["vo"], ["nv0"])
+    cp(T.nu[:], T.iw[:].indirect(col("uo", 0)), IW + ["uo"], ["nu"])
+    cp(full("Gu"), T.lti[:].indirect(col("uo", 0)), ["lti", "lti0", "uo"], ["Gu"])
+    act(full("fu"), full("Gu"), ACT.Relu, ["Gu"], ["fu"], bias=-float(NR - 1))
+    op("V", lambda: V.tensor_copy(T.Lw[:, SH:NL], T.lti[:, SH:NL]), ["lti", "Lw0", "Lwn"], ["L"])
+    mm("PD1", full("PD1"), [(T.I16[:], T.nv[:, 0:E], ["I16", "nv0"])], stop=False)
+    first_free("PM0", "fu")
+    act(full("ma0"), full("PM0"), ACT.Relu, ["PM0"], ["ma0"])
+    mm("PM1", full("PM1"), u_terms(0))
+    mm("PM2", full("PM2"), [(T.I16[:], T.nu[:], ["I16", "nu"]), (T.IB[:], full("ma0"), ["IB", "ma0"])])
+    act(full("Xu"), full("PM1"), ACT.Relu, ["PM1"], ["Xu"], bias=float(NR) - BIG)
+    act(full("Zu"), full("PM2"), ACT.Relu, ["PM2"], ["Zu"], bias=float(NL) - BIG)
+    colours_out(0, "PM0")
+    mm("PD0", full("PD0"), [(T.O16[:], full("KR"), ["O16", "KR"]), (T.nI32[:], full("Zu"), ["nI32", "Zu"])], stop=False)
+    colours_store(0, "PM0")
+    cp(T.nv[:, E:2 * E], T.iw[:].indirect(col("vo", 1)), IW + ["vo"], ["nv1"])
+    scatter_u(0)
+
+    for k in range(4):
+        r = [x for x in rts if x[2] == core and x[3] == k][0]
+        n = len(topo.engines(r[1], core))
+        count["arr%d" % k] = n
+        writer["land%d" % k] = ("arr%d" % k, n)
+        src, dst = T.land[:, k * CH:(k + 1) * CH], T.Rr[:, k * CH:(k + 1) * CH]
+        if k % 2 == 0:
+            ts(dst, src, float(SH), None, ALU.add, None, ["land%d" % k], ["Rr%d" % k])
+        else:
+            b = "PM%d" % (1 + k // 2)
+            mm(b, T[b][:, 0:CH], [(T.I16[:], src, ["I16", "land%d" % k])])
+            act(dst, T[b][:, 0:CH], ACT.Identity, [b], ["Rr%d" % k], bias=float(SH))
+    RR = ["Rr0", "Rr1", "Rr2", "Rr3", "Rrn"]
+    dma("S", "dC", T.Rw[:, 0:W + 8], T.Rr[:], RR, ["R"])
+
+    def table(t, i):
+        if i % 2:
+            return Lg, ["L"]
+        return (T.Rr[:], RR) if t == 0 else (T.Rw[:, 0:W + 8], ["R"])
+
+    def offs(t, i):
+        return (col("vo", t), "vo") if i == 0 else (col("xo", i), "xo%d" % i)
+
+    bank_of = {}
+
+    def step(t, i):
+        win, keys = table(t, i)
+        o, ok = offs(t, i)
+        m = ("mb%d" if i % 2 else "ma%d") % t
+        tt(full("H%d" % i), win.indirect(o), full(m), ALU.mult, keys + [ok, m], ["H%d" % i])
+
+    def spread(i):
+        b = "PX%d" % (px[0] % 3)
+        px[0] += 1
+        bank_of[i + 1] = b
+        terms = [(T.I16[:], T.KE[:], ["I16", "KE"])]
+        for j in range(16):
+            terms.append((T.B16[:, 15 - j:143 - j], T["H%d" % i][:, j:E:16], ["B16", "H%d" % i]))
+        mm(b, T[b][:, 0:K], terms)
+
+    def take(i):
+        b = bank_of[i]
+        cp(col("xo", i), T[b][:, 0:K], [b], ["xo%d" % i])
+
+    def steep(i):
+        b = bank_of[i]
+        bias = "bL" if i % 2 else "bR"
+        act(col("tt", i), T[b][:, 0:K], ACT.Identity, [b, bias], ["tt%d" % i], bias=T[bias][:], scale=1024.0)
+
+    def spare(i):
+        b = bank_of[i]
+        tt(col("mx", i), T[b][:, 0:K], col("tt", i), ALU.max, [b, "tt%d" % i], ["mx%d" % i])
+
+    def spare2(i):
+        cp(col("so", i), col("mx", i), ["mx%d" % i], ["so%d" % i])
+
+    def column(t, i):
+        win, keys = table(t, i)
+        o, ok = offs(t, i)
+        act(full("G%d" % i), win.indirect(o), ACT.Identity, keys + [ok], ["G%d" % i])
+
+    def diff(bank, plus, minus, start=True):
+        terms = []
+        if plus:
+            terms.append((T.O16[:], full(plus), ["O16", plus]))
+        if minus:
+            terms.append((T.nO16[:], full(minus), ["nO16", minus]))
+        mm(bank, full(bank), terms, start=start)
+
+    def change_left(t, i, bank):
+        tt(full("E%d" % i), full(bank), full("sg%d" % t), ALU.mult, [bank, "sg%d" % t], ["E%d" % i])
+
+    def scatter_left(i, a=0, b=K):
+        tt(Ls.indirect(col("so", i, a, b)), full("G%d" % i, a, b), full("E%d" % i, a, b), ALU.add,
+           ["so%d" % i, "G%d" % i, "E%d" % i], ["L"])
+
+    def change_right(bank):
+        tt(full(bank), full(bank), full("sg0"), ALU.mult, [bank, "sg0"], [])
+
+    def new_right(i, bank):
+        tt(full("E%d" % i), full(bank), full("G%d" % i), ALU.add, [bank, "G%d" % i], ["E%d" % i])
+
+    def scatter_right(i):
+        o, ok = (col("vo", 0), "vo") if i == 0 else (col("so", i), "so%d" % i)
+        op("A", lambda: A.activation(T.Rw[:].indirect(o), full("E%d" % i), ACT.Silu), [ok, "E%d" % i], ["R"])
+
+    def free_right(t):
+        win, keys = table(t, 0)
+        act(full("sv"), win.indirect(col("vo", t)), ACT.Sign, keys + ["vo"], ["sv"], bias=0.5 - NL)
+
+    def signs(t, bank):
+        mm(bank, full(bank), [(T.I2b[:], full("ma%d" % t), ["I2b", "ma%d" % t]), (T.nIb[:], full("mb%d" % t), ["nIb", "mb%d" % t])])
+        act(full("sg%d" % t), full(bank), ACT.Sign, [bank], ["sg%d" % t])
+
+    step(0, 0); free_right(0); first_free("PM1", "sv"); spread(0)
+    ts(full("mb0"), full("PM1"), T.cf[:], None, ALU.is_gt, None, ["PM1", "cf"], ["mb0"])
+    column(0, 0)
+    take(1); signs(0, "PM2"); diff("PD0", None, "H0", start=False)
+    step(0, 1); steep(1); column(0, 1); spread(1); diff("PD1", "H1", None, start=False)
+    change_right("PD0"); spare(1); new_right(0, "PD0")
+    take(2); spare2(1); step(0, 2); steep(2); column(0, 2); scatter_right(0); spread(2); diff("PD0", "H0", "H2")
+    change_left(0, 1, "PD1"); spare(2); scatter_left(1)
+    take(3); spare2(2); step(0, 3); steep(3); column(0, 3); spread(3); diff("PD1", "H3", "H1")
+    change_right("PD0"); spare(3); new_right(2, "PD0")
+    take(4); spare2(3); step(0, 4); steep(4); column(0, 4); scatter_right(2); spread(4); diff("PD0", "H2", "H4")
+    change_left(0, 3, "PD1"); diff("PD1", "KL", "H3"); spare(4); scatter_left(3)
+    take(5); steep(5); column(0, 5); spare2(4); change_right("PD0"); spare(5); change_left(0, 5, "PD1"); spare2(5)
+    new_right(4, "PD0"); scatter_right(4); scatter_left(5)
+
+    ts(full("fu"), Lg.indirect(col("uo", 1)), float(NR), None, ALU.is_equal, None, ["L", "uo"], ["fu"])
+    free_right(1)
+    act(full("Gu"), Lg.indirect(col("uo", 1)), ACT.Identity, ["L", "uo"], ["Gu"])
+    mm("PD0", full("PD0"), [(T.I16[:], T.nv[:, E:2 * E], ["I16", "nv1"])], stop=False)
+    first_free("PM0", "fu")
+    ts(full("ma1"), full("PM0"), 0.0, None, ALU.max, None, ["PM0"], ["ma1"])
+    mm("PM2", full("PM2"), u_terms(1))
+    first_free("PM1", "sv")
+    step(1, 0)
+    act(full("Xu"), full("PM2"), ACT.Relu, ["PM2"], ["Xu"], bias=float(NR) - BIG)
+    act(full("mb1"), full("PM1"), ACT.Relu, ["PM1", "bM"], ["mb1"], bias=T.bM[:], scale=0.5)
+    spread(0); scatter_u(1, 0, 14)
+    take(1); step(1, 1); steep(1); column(1, 1); spread(1); diff("PD0", "H1", None, start=False)
+    signs(1, "PM2"); colours_out(1, "PM0"); colours_store(1, "PM0")
+    spare(1); scatter_u(1, 14, K)
+    take(2); spare2(1); step(1, 2); spread(2); change_left(1, 1, "PD0"); scatter_left(1, 0, 10)
+    take(3); step(1, 3); steep(3); column(1, 3); spread(3); diff("PD1", "H3", "H1"); diff("PD0", "KL", "H3")
+    spare(3); scatter_left(1, 10, K)
+    take(4); spare2(3); step(1, 4); spread(4); change_left(1, 3, "PD1"); change_left(1, 5, "PD0"); scatter_left(3)
+    take(5); column(1, 5)
+    ts(col("tt", 5), T[bank_of[5]][:, 0:K], 1024.0, T.bL[:], ALU.mult, ALU.add, [bank_of[5], "bL"], ["tt5"])
+    spare(5); spare2(5); scatter_left(5)
+    dma("S", "dO", T.yl[:], T.Lw[:, SH:NL], ["L"], [])
+    wait("G", [(s, v) for s, v in count.items()])

@@ -8,41 +8,47 @@ LW, RW = 1768, 1736
 BIG = 2048.0
 CH = W // 4
 WORLD = 256
+BANKS = ((0, 512), (512, 1024), (1024, W))
 
 SCRATCH = {
     "rti": ("sbuf", [128, W], "int32"), "rtu": ("sbuf", [128, W], "float16"),
     "hop": ("sbuf", [128, CH], "float16"), "land": ("sbuf", [128, W], "float16"),
-    "lti": ("sbuf", [128, NL], "int32"), "Lw": ("sbuf", [128, LW], "float32"),
+    "lti": ("sbuf", [128, NL + 8], "int32"), "Lw": ("sbuf", [128, NL + 8], "float32"),
+    "DL0": ("sbuf", [128, LW], "float32"), "DL1": ("sbuf", [128, LW], "float32"),
     "Rr": ("sbuf", [128, W + 8], "float32"), "Rw": ("sbuf", [128, RW], "float32"),
     "eui": ("sbuf", [128, 2 * K], "int32"), "evi": ("sbuf", [128, 2 * K], "int32"),
     "uo": ("sbuf", [128, 2 * K], "uint16"), "vo": ("sbuf", [128, 2 * K], "uint16"),
     "iw": ("sbuf", [128, NL], "float32"),
     "nv": ("sbuf", [128, 2 * E], "float16"), "nu": ("sbuf", [128, E], "float16"),
     "xo": ("sbuf", [128, 6 * K], "uint16"), "so": ("sbuf", [128, 6 * K], "uint16"),
-    "tt": ("sbuf", [128, 6 * K], "float32"), "mx": ("sbuf", [128, 6 * K], "float32"),
-    "Gu": ("sbuf", [128, E], "float32"), "Xu": ("sbuf", [128, E], "float32"), "Zu": ("sbuf", [128, E], "float32"),
+    "zz": ("sbuf", [128, 6 * K], "float32"), "mx": ("sbuf", [128, 6 * K], "float32"),
+    "DU": ("sbuf", [128, NL], "float32"), "D16": ("sbuf", [128, W], "float16"), "L16": ("sbuf", [128, W], "float16"),
+    "Wu": ("sbuf", [128, E], "float32"), "Xu": ("sbuf", [128, E], "float32"), "Zu": ("sbuf", [128, E], "float16"),
     "fu": ("sbuf", [128, E], "bfloat16"), "sv": ("sbuf", [128, E], "bfloat16"),
     "yas": ("sbuf", [128, 2 * E], "float32"),
-    "ones": ("sbuf", [128, 128], "float32"), "Oa": ("sbuf", [128, 128], "float32"), "O32": ("sbuf", [128, 128], "float32"),
-    "I32": ("sbuf", [128, 128], "float32"), "T32": ("sbuf", [128, 128], "float32"), "nI32": ("sbuf", [128, 128], "float32"),
+    "ji": ("sbuf", [128, 128], "int32"), "jg": ("sbuf", [128, 128], "int32"), "Tl": ("sbuf", [128, 128], "float16"),
     "O16": ("sbuf", [128, 128], "float16"), "nO16": ("sbuf", [128, 128], "float16"), "I16": ("sbuf", [128, 128], "float16"),
-    "B16": ("sbuf", [128, 144], "float16"), "KE": ("sbuf", [128, K], "float16"), "kf": ("sbuf", [128, K], "float32"),
-    "KL": ("sbuf", [128, E], "float16"), "KR": ("sbuf", [128, E], "float16"),
-    "Mb": ("sbuf", [128, 128], "bfloat16"), "IB": ("sbuf", [128, 128], "bfloat16"), "I2b": ("sbuf", [128, 128], "bfloat16"),
-    "nIb": ("sbuf", [128, 128], "bfloat16"), "Yw": ("sbuf", [128, 8], "bfloat16"),
-    "pi": ("sbuf", [128, 1], "int32"), "ci": ("sbuf", [128, 1], "int32"), "cf": ("sbuf", [128, 1], "float32"),
+    "nI16": ("sbuf", [128, 128], "float16"), "I2": ("sbuf", [128, 128], "float16"), "IB": ("sbuf", [128, 128], "float16"),
+    "Mb": ("sbuf", [128, 128], "float16"), "MB": ("sbuf", [128, 128], "float16"),
+    "B16": ("sbuf", [128, 144], "float16"), "KE": ("sbuf", [128, K], "float16"),
+    "KL": ("sbuf", [128, E], "float16"), "KR": ("sbuf", [128, E], "float16"), "Yw": ("sbuf", [128, 8], "float16"),
+    "pi": ("sbuf", [128, 1], "int32"), "ci": ("sbuf", [128, 1], "int32"), "gi": ("sbuf", [128, 1], "int32"),
+    "cf": ("sbuf", [128, 1], "float32"), "pf": ("sbuf", [128, 1], "float32"), "gf": ("sbuf", [128, 1], "float32"),
     "bL": ("sbuf", [128, 1], "float32"), "bR": ("sbuf", [128, 1], "float32"), "bM": ("sbuf", [128, 1], "float32"),
     "nn": ("sbuf", [128, 8], "float32"),
 }
 for _i in range(5):
     SCRATCH["H%d" % _i] = ("sbuf", [128, E], "float16")
+for _i in (0, 2, 4):
+    SCRATCH["G%d" % _i] = ("sbuf", [128, E], "float16")
+    SCRATCH["E%d" % _i] = ("sbuf", [128, E], "float16")
 for _i in range(6):
-    SCRATCH["G%d" % _i] = ("sbuf", [128, E], "float32")
-    SCRATCH["E%d" % _i] = ("sbuf", [128, E], "float32")
+    SCRATCH["N%d" % _i] = ("sbuf", [128, E], "float32")
 for _t in range(2):
-    for _n in ("ma", "mb", "sg"):
-        SCRATCH["%s%d" % (_n, _t)] = ("sbuf", [128, E], "bfloat16")
-for _n in ("PX0", "PX1", "PX2", "PD0", "PD1", "PM0", "PM1", "PM2"):
+    SCRATCH["ma%d" % _t] = ("sbuf", [128, E], "float16")
+    SCRATCH["mb%d" % _t] = ("sbuf", [128, E], "float16")
+    SCRATCH["sg%d" % _t] = ("sbuf", [128, E], "float32")
+for _n in ("PX0", "PX1", "PA", "PB", "PC", "PL0", "PL1", "PL2"):
     SCRATCH[_n] = ("psum", [128, 512], "float32")
 
 SEMAPHORES = ["sV", "sA", "sP", "sG", "hopin", "sent", "arr0", "arr1", "arr2", "arr3",
@@ -160,62 +166,55 @@ def rank_program(g, core, T, topo):
     def act(out, in_, func, rd, wr, bias=0.0, scale=1.0):
         op("A", lambda: A.activation(out, in_, func, bias=bias, scale=scale), rd, wr)
 
+    def iota(out, step, n, cm, key):
+        op("G", lambda: g.iota(out, [[step, n]], 0, cm, allow_small_or_imprecise_dtypes=True), [], [key])
+
     def col(buf, i, a=0, b=K):
         return T[buf][:, i * K + a:i * K + b]
 
     def full(name, a=0, b=K):
         return T[name][:, 16 * a:16 * b]
 
+    def lin(bank, terms, start=True, stop=True):
+        mm(bank, full(bank), [(T[m][:], full(x) if isinstance(x, str) else x[0], [m, x if isinstance(x, str) else x[1]])
+                              for m, x in terms], start, stop)
+
+    NV = [(T.nv[:, t * E:(t + 1) * E], "nv%d" % t) for t in range(2)]
+
     h = W // 2
     dma("S", "dR0", T.rti[:, 0:h], T.rt[:, 0:h], [], ["rti0"])
     dma("S", "dR1", T.rti[:, h:W], T.rt[:, h:W], [], ["rti1"])
+    dma("S", "dU", T.eui[:], T.eu[:], [], ["eui"])
+    dma("S", "dV", T.evi[:], T.ev[:], [], ["evi"])
     dma("S", "dL", T.lti[:, SH:NL], T.lt[:], [], ["lti"])
-    dma("A", "dU", T.eui[:], T.eu[:], [], ["eui"])
-    dma("A", "dV", T.evi[:], T.ev[:], [], ["evi"])
 
-    fill(T.ones[:], 1.0, "ones")
+    iota(T.pi[:], 0, 1, 1, "pi")
+    iota(T.ji[:], 1, 128, 0, "ji")
     fill(T.nn[:], float(NL), "nn")
-    op("G", lambda: g.iota(T.pi[:], [[0, 1]], 0, 1), [], ["pi"])
-    op("G", lambda: g.iota(T.kf[:], [[1, K]], 0, 0, allow_small_or_imprecise_dtypes=True), [], ["kf"])
-    op("G", lambda: g.affine_select(T.Oa[:], T.ones[:], [[-16, 8], [0, 16]], ALU.is_ge, 0.0, 0, 1), ["ones"], ["Oa"])
-    op("G", lambda: g.affine_select(T.I32[:], T.ones[:], [[-1, 128]], ALU.is_equal, 0.0, 0, 1), ["ones"], ["I32"])
-    op("G", lambda: g.affine_select(T.O32[:], T.Oa[:], [[16, 8], [0, 16]], ALU.is_ge, 0.0, 15, -1), ["Oa"], ["O32"])
-    q4 = NL // 4
-    op("G", lambda: g.iota(T.iw[:, 0:q4], [[-1, q4]], 0, 0, allow_small_or_imprecise_dtypes=True), [], ["iw0"])
-    op("G", lambda: g.affine_select(T.T32[:], T.O32[:], [[1, 128]], ALU.is_gt, 0.0, 0, -1), ["O32"], ["T32"])
     act(T.Rr[:, W:W + 8], T.nn[:], ACT.Silu, ["nn"], ["Rrn"])
     fill(T.B16[:], 0.0, "B16")
-    fill(T.KL[:], W / 16.0, "KL")
+    fill(T.KL[:], NR / 16.0, "KL")
     fill(T.KR[:], NL / 16.0, "KR")
     fill(T.lti[:, 0:SH], 0, "lti0")
+    fill(T.lti[:, NL:NL + 8], NR, "ltin")
     fill(T.Lw[:, 0:SH], 0.0, "Lw0")
     fill(T.Lw[:, NL:NL + 8], float(NR), "Lwn")
     ts(T.ci[:], T.pi[:], 15, None, ALU.bitwise_and, None, ["pi"], ["ci"])
-    ts(T.KE[:], T.kf[:], 1.0 / 1024, None, ALU.mult, None, ["kf"], ["KE"])
+    ts(T.gi[:], T.pi[:], 4, None, ALU.arith_shift_right, None, ["pi"], ["gi"])
+    cp(T.pf[:], T.pi[:], ["pi"], ["pf"])
     cp(T.cf[:], T.ci[:], ["ci"], ["cf"])
-    cp(T.I16[:], T.I32[:], ["I32"], ["I16"])
-    ts(T.bL[:], T.cf[:], float(K), float(NL + 1 - 1024 * NL), ALU.mult, ALU.add, ["cf"], ["bL"])
-    ts(T.bR[:], T.cf[:], float(K), float(NR + 1 - 1024 * NR), ALU.mult, ALU.add, ["cf"], ["bR"])
-    ts(T.bM[:], T.cf[:], -0.5, 0.5, ALU.mult, ALU.add, ["cf"], ["bM"])
-    ts(T.uo[:], T.eui[:], float(SH), None, ALU.add, None, ["eui"], ["uo"])
-    cp(T.vo[:], T.evi[:], ["evi"], ["vo"])
-    cp(T.O16[:], T.O32[:], ["O32"], ["O16"])
-    ts(T.nO16[:], T.O32[:], -1.0, None, ALU.mult, None, ["O32"], ["nO16"])
-    cp(T.B16[:, 15:143:16], T.O32[:, 0:128:16], ["O32", "B16"], ["B16"])
-    act(T.IB[:], T.I32[:], ACT.Identity, ["I32"], ["IB"], scale=BIG)
-    act(T.nI32[:], T.I32[:], ACT.Identity, ["I32"], ["nI32"], scale=-1.0)
-    act(T.iw[:, q4:2 * q4], T.iw[:, 0:q4], ACT.Identity, ["iw0"], ["iw1"], bias=-float(q4))
-    act(T.iw[:, 2 * q4:3 * q4], T.iw[:, 0:q4], ACT.Identity, ["iw0"], ["iw2"], bias=-float(2 * q4))
-    act(T.iw[:, 3 * q4:NL], T.iw[:, 0:q4], ACT.Identity, ["iw0"], ["iw3"], bias=-float(3 * q4))
-    act(T.I2b[:], T.I32[:], ACT.Identity, ["I32"], ["I2b"], scale=2.0)
-    act(T.nIb[:], T.I32[:], ACT.Identity, ["I32"], ["nIb"], scale=-1.0)
-    act(T.Yw[:], T.O32[:, 0:128:16], ACT.Identity, ["O32", "cf"], ["Yw"], scale=T.cf[:])
-    IW = ["iw0", "iw1", "iw2", "iw3"]
+    cp(T.gf[:], T.gi[:], ["gi"], ["gf"])
+    ts(T.jg[:], T.ji[:], 4, None, ALU.arith_shift_right, None, ["ji"], ["jg"])
+    ts(T.I16[:], T.ji[:], T.pf[:], None, ALU.is_equal, None, ["ji", "pf"], ["I16"])
+    ts(T.O16[:], T.jg[:], T.gf[:], None, ALU.is_equal, None, ["jg", "gf"], ["O16"])
+    ts(T.Tl[:], T.ji[:], T.pf[:], -1.0, ALU.is_gt, ALU.mult, ["ji", "pf"], ["Tl"])
 
     mine = [r for r in rts if r[0] == core]
     for half in range(2):
-        cp(T.rtu[:, half * h:(half + 1) * h], T.rti[:, half * h:(half + 1) * h], ["rti%d" % half], ["rtu%d" % half])
-        wait("G", [writer["rtu%d" % half]])
+        a, b, c_ = half * h, half * h + CH, (half + 1) * h
+        cp(T.rtu[:, a:b], T.rti[:, a:b], ["rti%d" % half], ["rtu%d" % (2 * half)])
+        act(T.rtu[:, b:c_], T.rti[:, b:c_], ACT.Identity, ["rti%d" % half], ["rtu%d" % (2 * half + 1)])
+        wait("G", [writer["rtu%d" % (2 * half)], writer["rtu%d" % (2 * half + 1)]])
         trs = []
         for s, c, d, k, eng in mine[2 * half:2 * half + 2]:
             rid, pid = topo.addr(c, core)
@@ -223,44 +222,86 @@ def rank_program(g, core, T, topo):
                                          src=T.rtu[:, k * CH:(k + 1) * CH], dst=T.hop[:]))
             count["sent"] = count.get("sent", 0) + len(eng)
         g.remote_dma_fused(trs, local_sem=T.sem.sent)
-    tt(T.Mb[:], T.I32[:], T.T32[:], ALU.subtract, ["I32", "T32"], ["Mb"])
+    iota(T.DL0[:, 0:NL], 0, NL, 0, "DL0")
+    iota(T.DU[:, SH:NL], 0, W, 0, "DU")
+    iota(T.DL1[:, SH:NL], 0, W, 0, "DL1")
 
-    Lg, Ls = T.Lw[:, 0:NL + 8], T.Lw[:]
-    px = [0]
+    act(T.iw[:, 0:128], T.ji[:], ACT.Identity, ["ji"], ["iw"], scale=-1.0)
+    n = 128
+    while n < NL:
+        m = min(n, NL - n)
+        act(T.iw[:, n:n + m], T.iw[:, 0:m], ACT.Identity, ["iw"], ["iw"], bias=-float(n))
+        n += m
+    tt(T.Tl[:], T.Tl[:], T.O16[:], ALU.mult, ["Tl", "O16"], ["Tl"])
+    ts(T.uo[:], T.eui[:], float(SH), None, ALU.add, None, ["eui"], ["uo"])
+    cp(T.vo[:], T.evi[:], ["evi"], ["vo"])
+    tt(T.Mb[:], T.Tl[:], T.I16[:], ALU.add, ["Tl", "I16"], ["Mb"])
+    ts(T.KE[:], T.ji[:, 0:K], 1.0 / 1024, None, ALU.mult, None, ["ji"], ["KE"])
+    ts(T.IB[:], T.I16[:], BIG, None, ALU.mult, None, ["I16"], ["IB"])
+    ts(T.MB[:], T.Mb[:], BIG, None, ALU.mult, None, ["Mb"], ["MB"])
+    ts(T.nO16[:], T.O16[:], -1.0, None, ALU.mult, None, ["O16"], ["nO16"])
+    ts(T.nI16[:], T.I16[:], -1.0, None, ALU.mult, None, ["I16"], ["nI16"])
+    ts(T.I2[:], T.I16[:], 2.0, None, ALU.mult, None, ["I16"], ["I2"])
+    ts(T.Yw[:], T.O16[:, 0:128:16], T.cf[:], None, ALU.mult, None, ["O16", "cf"], ["Yw"])
+    cp(T.B16[:, 15:143:16], T.O16[:, 0:128:16], ["O16", "B16"], ["B16"])
+    ts(T.bL[:], T.cf[:], float(K), float(NL + 1 - 1024 * NL), ALU.mult, ALU.add, ["cf"], ["bL"])
+    ts(T.bR[:], T.cf[:], float(K), float(NR + 1 - 1024 * NR), ALU.mult, ALU.add, ["cf"], ["bR"])
+    ts(T.bM[:], T.cf[:], -0.5, 0.5, ALU.mult, ALU.add, ["cf"], ["bM"])
 
-    def u_terms(t):
-        return [(T.I16[:], T.nv[:, t * E:(t + 1) * E], ["I16", "nv%d" % t]), (T.IB[:], full("ma%d" % t), ["IB", "ma%d" % t])]
+    LT = ["lti", "lti0", "ltin"]
+    LN = ["L0", "L1", "L2", "Lw0", "Lwn"]
 
-    def first_free(bank, flags):
-        mm(bank, full(bank), [(T.Mb[:], full(flags), ["Mb", flags])])
-
-    def colours_out(t, bank):
+    def colours(t, bank):
         mm(bank, T[bank][0:8, 0:E], [(T.Yw[:], full("ma%d" % t), ["Yw", "ma%d" % t])])
-
-    def colours_store(t, bank):
         act(T.yas[0:8, t * E:(t + 1) * E], T[bank][0:8, 0:E], ACT.Copy, [bank], ["yas%d" % t])
         dma("S", "dY%d" % t, T.ya[:, t * E:(t + 1) * E], T.yas[0:8, t * E:(t + 1) * E], ["yas%d" % t], [])
 
     def scatter_u(t, a=0, b=K):
-        tt(Ls.indirect(col("uo", t, a, b)), full("Gu", a, b), full("Xu", a, b), ALU.subtract, ["uo", "Gu", "Xu"], ["L"])
+        d = "DL%d" % t
+        ts(T[d][:].indirect(col("uo", t, a, b)), full("Xu", a, b), -1.0, 0.0, ALU.mult, ALU.add, ["uo", "Xu"], [d])
 
-    cp(T.nv[:, 0:E], T.iw[:].indirect(col("vo", 0)), IW + ["vo"], ["nv0"])
-    cp(T.nu[:], T.iw[:].indirect(col("uo", 0)), IW + ["uo"], ["nu"])
-    cp(full("Gu"), T.lti[:].indirect(col("uo", 0)), ["lti", "lti0", "uo"], ["Gu"])
-    act(full("fu"), full("Gu"), ACT.Relu, ["Gu"], ["fu"], bias=-float(NR - 1))
-    op("V", lambda: V.tensor_copy(T.Lw[:, SH:NL], T.lti[:, SH:NL]), ["lti", "Lw0", "Lwn"], ["L"])
-    mm("PD1", full("PD1"), [(T.I16[:], T.nv[:, 0:E], ["I16", "nv0"])], stop=False)
-    first_free("PM0", "fu")
-    act(full("ma0"), full("PM0"), ACT.Relu, ["PM0"], ["ma0"])
-    mm("PM1", full("PM1"), u_terms(0))
-    mm("PM2", full("PM2"), [(T.I16[:], T.nu[:], ["I16", "nu"]), (T.IB[:], full("ma0"), ["IB", "ma0"])])
-    act(full("Xu"), full("PM1"), ACT.Relu, ["PM1"], ["Xu"], bias=float(NR) - BIG)
-    act(full("Zu"), full("PM2"), ACT.Relu, ["PM2"], ["Zu"], bias=float(NL) - BIG)
-    colours_out(0, "PM0")
-    mm("PD0", full("PD0"), [(T.O16[:], full("KR"), ["O16", "KR"]), (T.nI32[:], full("Zu"), ["nI32", "Zu"])], stop=False)
-    colours_store(0, "PM0")
-    cp(T.nv[:, E:2 * E], T.iw[:].indirect(col("vo", 1)), IW + ["vo"], ["nv1"])
+    def change_u(t, bank, by=1.0):
+        lin(bank, [("I16", NV[t]), ("MB", "fu")])
+        act(full("Xu"), full(bank), ACT.Relu, [bank], ["Xu"], bias=(NR - BIG) * by, scale=by)
+
+    def narrow(k):
+        a, b = BANKS[k]
+        act(T.L16[:, a:b], T.Lw[:, SH + a:SH + b], ACT.Identity, ["L%d" % k], ["L16%d" % k])
+
+    def narrow_u(k):
+        a, b = BANKS[k]
+        act(T.D16[:, a:b], T.DU[:, SH + a:SH + b], ACT.Identity, ["DU"], ["D16%d" % k], scale=-1.0 / SH)
+
+    def hold_sum(k):
+        a, b = BANKS[k]
+        mm("PL%d" % k, T["PL%d" % k][:, 0:b - a], [(T.I16[:], T.L16[:, a:b], ["I16", "L16%d" % k]),
+                                                   (T.I16[:], T.D16[:, a:b], ["I16", "D16%d" % k])])
+
+    def hold(k, src, keys):
+        a, b = BANKS[k]
+        act(T["PL%d" % k][:, 0:b - a], src[:, SH + a:SH + b], ACT.Identity, keys, ["PL%d" % k])
+
+    def merge(t, k, a=None, b=None):
+        a0, b0 = BANKS[k]
+        a, b = (a0, b0) if a is None else (a, b)
+        tt(T.Lw[:, SH + a:SH + b], T["DL%d" % t][:, SH + a:SH + b], T["PL%d" % k][:, a - a0:b - a0], ALU.add,
+           ["DL%d" % t, "PL%d" % k], ["L%d" % k])
+
+    cp(NV[0][0], T.iw[:].indirect(col("vo", 0)), ["iw", "vo"], ["nv0"])
+    cp(T.nu[:], T.iw[:].indirect(col("uo", 0)), ["iw", "uo"], ["nu"])
+    act(full("fu"), T.lti[:].indirect(col("uo", 0)), ACT.Relu, LT + ["uo"], ["fu"], bias=-float(NR - 1))
+    cp(NV[1][0], T.iw[:].indirect(col("vo", 1)), ["iw", "vo"], ["nv1"])
+    ts(full("Wu"), T.lti[:].indirect(col("uo", 1)), -1.0, float(NR), ALU.mult, ALU.add, LT + ["uo"], ["Wu"])
+    change_u(0, "PA")
+    lin("PB", [("Mb", "fu")])
+    act(full("ma0"), full("PB"), ACT.Relu, ["PB"], ["ma0"])
+    lin("PC", [("I16", "nu"), ("MB", "fu")])
     scatter_u(0)
+    act(full("Zu"), full("PC"), ACT.Relu, ["PC"], ["Zu"], bias=float(NL) - BIG)
+    colours(0, "PB")
+    for k in range(3):
+        hold(k, T.lti, ["lti"])
+    lin("PA", [("O16", "KR"), ("nI16", "Zu")], stop=False)
 
     for k in range(4):
         r = [x for x in rts if x[2] == core and x[3] == k][0]
@@ -271,21 +312,20 @@ def rank_program(g, core, T, topo):
         if k % 2 == 0:
             ts(dst, src, float(SH), None, ALU.add, None, ["land%d" % k], ["Rr%d" % k])
         else:
-            b = "PM%d" % (1 + k // 2)
-            mm(b, T[b][:, 0:CH], [(T.I16[:], src, ["I16", "land%d" % k])])
-            act(dst, T[b][:, 0:CH], ACT.Identity, [b], ["Rr%d" % k], bias=float(SH))
+            act(dst, src, ACT.Identity, ["land%d" % k], ["Rr%d" % k], bias=float(SH))
     RR = ["Rr0", "Rr1", "Rr2", "Rr3", "Rrn"]
     dma("S", "dC", T.Rw[:, 0:W + 8], T.Rr[:], RR, ["R"])
 
     def table(t, i):
         if i % 2:
-            return Lg, ["L"]
+            return (T.lti[:], LT) if t == 0 else (T.Lw[:], LN)
         return (T.Rr[:], RR) if t == 0 else (T.Rw[:, 0:W + 8], ["R"])
 
     def offs(t, i):
         return (col("vo", t), "vo") if i == 0 else (col("xo", i), "xo%d" % i)
 
-    bank_of = {}
+    def bank(i):
+        return "PX%d" % (i % 2)
 
     def step(t, i):
         win, keys = table(t, i)
@@ -293,105 +333,109 @@ def rank_program(g, core, T, topo):
         m = ("mb%d" if i % 2 else "ma%d") % t
         tt(full("H%d" % i), win.indirect(o), full(m), ALU.mult, keys + [ok, m], ["H%d" % i])
 
-    def spread(i):
-        b = "PX%d" % (px[0] % 3)
-        px[0] += 1
-        bank_of[i + 1] = b
+    def spread(i, stop=True):
+        b = bank(i + 1)
         terms = [(T.I16[:], T.KE[:], ["I16", "KE"])]
         for j in range(16):
             terms.append((T.B16[:, 15 - j:143 - j], T["H%d" % i][:, j:E:16], ["B16", "H%d" % i]))
-        mm(b, T[b][:, 0:K], terms)
+        mm(b, T[b][:, 0:K], terms, stop=stop)
 
     def take(i):
-        b = bank_of[i]
-        cp(col("xo", i), T[b][:, 0:K], [b], ["xo%d" % i])
+        cp(col("xo", i), T[bank(i)][:, 0:K], [bank(i)], ["xo%d" % i])
 
-    def steep(i):
-        b = bank_of[i]
-        bias = "bL" if i % 2 else "bR"
-        act(col("tt", i), T[b][:, 0:K], ACT.Identity, [b, bias], ["tt%d" % i], bias=T[bias][:], scale=1024.0)
+    def ended(i, e="A"):
+        b, bias = bank(i), "bL" if i % 2 else "bR"
+        if e == "A":
+            act(col("zz", i), T[b][:, 0:K], ACT.Identity, [b, bias], ["zz%d" % i], bias=T[bias][:], scale=1024.0)
+        else:
+            ts(col("zz", i), T[b][:, 0:K], 1024.0, T[bias][:], ALU.mult, ALU.add, [b, bias], ["zz%d" % i])
 
     def spare(i):
-        b = bank_of[i]
-        tt(col("mx", i), T[b][:, 0:K], col("tt", i), ALU.max, [b, "tt%d" % i], ["mx%d" % i])
+        tt(col("mx", i), T[bank(i)][:, 0:K], col("zz", i), ALU.max, [bank(i), "zz%d" % i], ["mx%d" % i])
 
     def spare2(i):
         cp(col("so", i), col("mx", i), ["mx%d" % i], ["so%d" % i])
 
-    def column(t, i):
+    def column(t, i, e="A"):
         win, keys = table(t, i)
         o, ok = offs(t, i)
-        act(full("G%d" % i), win.indirect(o), ACT.Identity, keys + [ok], ["G%d" % i])
+        if e == "A":
+            act(full("G%d" % i), win.indirect(o), ACT.Identity, keys + [ok], ["G%d" % i])
+        else:
+            cp(full("G%d" % i), win.indirect(o), keys + [ok], ["G%d" % i])
 
-    def diff(bank, plus, minus, start=True):
-        terms = []
-        if plus:
-            terms.append((T.O16[:], full(plus), ["O16", plus]))
-        if minus:
-            terms.append((T.nO16[:], full(minus), ["nO16", minus]))
-        mm(bank, full(bank), terms, start=start)
+    def out(i, b):
+        act(full("N%d" % i), full(b), ACT.Identity, [b], ["N%d" % i])
 
-    def change_left(t, i, bank):
-        tt(full("E%d" % i), full(bank), full("sg%d" % t), ALU.mult, [bank, "sg%d" % t], ["E%d" % i])
+    def scatter_left(t, i, a=0, b=K):
+        d = "DL%d" % t
+        tt(T[d][:].indirect(col("so", i, a, b)), full("N%d" % i, a, b), full("sg%d" % t, a, b), ALU.mult,
+           ["so%d" % i, "N%d" % i, "sg%d" % t], [d])
 
-    def scatter_left(i, a=0, b=K):
-        tt(Ls.indirect(col("so", i, a, b)), full("G%d" % i, a, b), full("E%d" % i, a, b), ALU.add,
-           ["so%d" % i, "G%d" % i, "E%d" % i], ["L"])
+    def change_right(i, b):
+        tt(full("E%d" % i), full(b), full("sg0"), ALU.mult, [b, "sg0"], ["E%d" % i])
 
-    def change_right(bank):
-        tt(full(bank), full(bank), full("sg0"), ALU.mult, [bank, "sg0"], [])
-
-    def new_right(i, bank):
-        tt(full("E%d" % i), full(bank), full("G%d" % i), ALU.add, [bank, "G%d" % i], ["E%d" % i])
+    def new_right(i, b):
+        lin(b, [("I16", "G%d" % i), ("I16", "E%d" % i)])
 
     def scatter_right(i):
         o, ok = (col("vo", 0), "vo") if i == 0 else (col("so", i), "so%d" % i)
-        op("A", lambda: A.activation(T.Rw[:].indirect(o), full("E%d" % i), ACT.Silu), [ok, "E%d" % i], ["R"])
+        op("A", lambda: A.activation(T.Rw[:].indirect(o), full("N%d" % i), ACT.Silu), [ok, "N%d" % i], ["R"])
 
-    def free_right(t):
-        win, keys = table(t, 0)
-        act(full("sv"), win.indirect(col("vo", t)), ACT.Sign, keys + ["vo"], ["sv"], bias=0.5 - NL)
+    def signs(t, b):
+        lin(b, [("I2", "ma%d" % t), ("nI16", "mb%d" % t)])
+        act(full("sg%d" % t), full(b), ACT.Sign, [b], ["sg%d" % t])
 
-    def signs(t, bank):
-        mm(bank, full(bank), [(T.I2b[:], full("ma%d" % t), ["I2b", "ma%d" % t]), (T.nIb[:], full("mb%d" % t), ["nIb", "mb%d" % t])])
-        act(full("sg%d" % t), full(bank), ACT.Sign, [bank], ["sg%d" % t])
+    step(0, 0)
+    act(full("sv"), T.Rr[:].indirect(col("vo", 0)), ACT.Sign, RR + ["vo"], ["sv"], bias=0.5 - NL)
+    lin("PB", [("Mb", "sv")]); spread(0)
+    act(full("mb0"), full("PB"), ACT.Relu, ["PB", "bM"], ["mb0"], bias=T.bM[:], scale=0.5)
+    column(0, 0, "V"); take(1); step(0, 1); ended(1); signs(0, "PC"); lin("PA", [("nO16", "H0")], start=False)
+    lin("PB", [("I16", NV[0])], stop=False); spread(1); spare(1); lin("PB", [("O16", "H1")], start=False)
+    change_right(0, "PA"); spare2(1); new_right(0, "PC")
+    take(2); step(0, 2); ended(2); out(1, "PB"); out(0, "PC"); column(0, 2); scatter_right(0)
+    lin("PA", [("O16", "H0")], stop=False); spare(2); spread(2); lin("PA", [("nO16", "H2")], start=False)
+    scatter_left(0, 1, 0, 12); spare2(2)
+    take(3); ended(3, "V"); step(0, 3); spare(3); change_right(2, "PA")
+    lin("PB", [("nO16", "H1")], stop=False); spread(3); new_right(2, "PC"); lin("PB", [("O16", "H3")], start=False)
+    spare2(3); scatter_left(0, 1, 12, 18)
+    take(4); ended(4, "V"); step(0, 4)
+    out(2, "PC"); out(3, "PB"); column(0, 4); scatter_right(2)
+    lin("PA", [("O16", "H2")], stop=False); spare(4); lin("PA", [("nO16", "H4")], start=False); spread(4)
+    lin("PB", [("O16", "KL"), ("nO16", "H3")])
+    spare2(4); change_right(4, "PA"); new_right(4, "PC"); scatter_left(0, 1, 18, K)
+    ended(5, "V"); out(5, "PB"); out(4, "PC"); scatter_right(4)
+    scatter_left(0, 3, 0, 14); spare(5); scatter_left(0, 3, 14, K); spare2(5); scatter_left(0, 5)
 
-    step(0, 0); free_right(0); first_free("PM1", "sv"); spread(0)
-    ts(full("mb0"), full("PM1"), T.cf[:], None, ALU.is_gt, None, ["PM1", "cf"], ["mb0"])
-    column(0, 0)
-    take(1); signs(0, "PM2"); diff("PD0", None, "H0", start=False)
-    step(0, 1); steep(1); column(0, 1); spread(1); diff("PD1", "H1", None, start=False)
-    change_right("PD0"); spare(1); new_right(0, "PD0")
-    take(2); spare2(1); step(0, 2); steep(2); column(0, 2); scatter_right(0); spread(2); diff("PD0", "H0", "H2")
-    change_left(0, 1, "PD1"); spare(2); scatter_left(1)
-    take(3); spare2(2); step(0, 3); steep(3); column(0, 3); spread(3); diff("PD1", "H3", "H1")
-    change_right("PD0"); spare(3); new_right(2, "PD0")
-    take(4); spare2(3); step(0, 4); steep(4); column(0, 4); scatter_right(2); spread(4); diff("PD0", "H2", "H4")
-    change_left(0, 3, "PD1"); diff("PD1", "KL", "H3"); spare(4); scatter_left(3)
-    take(5); steep(5); column(0, 5); spare2(4); change_right("PD0"); spare(5); change_left(0, 5, "PD1"); spare2(5)
-    new_right(4, "PD0"); scatter_right(4); scatter_left(5)
-
-    ts(full("fu"), Lg.indirect(col("uo", 1)), float(NR), None, ALU.is_equal, None, ["L", "uo"], ["fu"])
-    free_right(1)
-    act(full("Gu"), Lg.indirect(col("uo", 1)), ACT.Identity, ["L", "uo"], ["Gu"])
-    mm("PD0", full("PD0"), [(T.I16[:], T.nv[:, E:2 * E], ["I16", "nv1"])], stop=False)
-    first_free("PM0", "fu")
-    ts(full("ma1"), full("PM0"), 0.0, None, ALU.max, None, ["PM0"], ["ma1"])
-    mm("PM2", full("PM2"), u_terms(1))
-    first_free("PM1", "sv")
-    step(1, 0)
-    act(full("Xu"), full("PM2"), ACT.Relu, ["PM2"], ["Xu"], bias=float(NR) - BIG)
-    act(full("mb1"), full("PM1"), ACT.Relu, ["PM1", "bM"], ["mb1"], bias=T.bM[:], scale=0.5)
-    spread(0); scatter_u(1, 0, 14)
-    take(1); step(1, 1); steep(1); column(1, 1); spread(1); diff("PD0", "H1", None, start=False)
-    signs(1, "PM2"); colours_out(1, "PM0"); colours_store(1, "PM0")
-    spare(1); scatter_u(1, 14, K)
-    take(2); spare2(1); step(1, 2); spread(2); change_left(1, 1, "PD0"); scatter_left(1, 0, 10)
-    take(3); step(1, 3); steep(3); column(1, 3); spread(3); diff("PD1", "H3", "H1"); diff("PD0", "KL", "H3")
-    spare(3); scatter_left(1, 10, K)
-    take(4); spare2(3); step(1, 4); spread(4); change_left(1, 3, "PD1"); change_left(1, 5, "PD0"); scatter_left(3)
-    take(5); column(1, 5)
-    ts(col("tt", 5), T[bank_of[5]][:, 0:K], 1024.0, T.bL[:], ALU.mult, ALU.add, [bank_of[5], "bL"], ["tt5"])
-    spare(5); spare2(5); scatter_left(5)
-    dma("S", "dO", T.yl[:], T.Lw[:, SH:NL], ["L"], [])
+    column(1, 0)
+    lin("PC", [("I16", NV[1])], stop=False)
+    lin("PA", [("I16", "G0")], stop=False)
+    tt(full("fu"), T.DL0[:, 0:NL].indirect(col("uo", 1)), full("Wu"), ALU.is_equal, ["DL0", "uo", "Wu"], ["fu"])
+    ts(full("sv"), full("G0"), float(NL), None, ALU.is_equal, None, ["G0"], ["sv"])
+    lin("PA", [("MB", "fu")], start=False)
+    act(full("H0"), full("PA"), ACT.Relu, ["PA"], ["H0"], bias=-BIG)
+    lin("PB", [("Mb", "sv")])
+    act(full("mb1"), full("PB"), ACT.Relu, ["PB"], ["mb1"])
+    lin("PC", [("MB", "fu")], start=False)
+    act(full("Xu"), full("PC"), ACT.Relu, ["PC"], ["Xu"], bias=(NR - BIG) * SH, scale=float(SH))
+    spread(0)
+    merge(0, 0); merge(0, 1); merge(0, 2)
+    ts(full("ma1"), full("H0"), 0.0, None, ALU.is_gt, None, ["H0"], ["ma1"])
+    take(1); ended(1, "V"); step(1, 1); signs(1, "PB")
+    lin("PA", [("I16", NV[1])], stop=False); spare(1); spread(1, True); lin("PA", [("O16", "H1")], start=False)
+    narrow(0); narrow(2); out(1, "PA"); spare2(1)
+    take(2); step(1, 2); spread(2)
+    op("A", lambda: A.activation(T.DU[:].indirect(col("uo", 1)), full("Xu"), ACT.Silu), ["uo", "Xu"], ["DU"])
+    scatter_left(1, 1, 0, 14)
+    take(3); ended(3, "V"); step(1, 3); narrow(1); narrow_u(0)
+    lin("PA", [("nO16", "H1")], stop=False); lin("PB", [("O16", "KL")], stop=False); spare(3); spread(3, True)
+    lin("PA", [("O16", "H3")], start=False); lin("PB", [("nO16", "H3")], start=False); out(3, "PA"); out(5, "PB")
+    scatter_left(1, 1, 14, K); spare2(3)
+    take(4); step(1, 4); narrow_u(1); narrow_u(2); hold_sum(0); spread(4)
+    scatter_left(1, 3, 0, 14); ended(5); hold_sum(1); hold_sum(2); colours(1, "PC")
+    scatter_left(1, 3, 14, 20); spare(5); scatter_left(1, 3, 20, K); spare2(5); scatter_left(1, 5)
+    for k in range(3):
+        a, b = BANKS[k]
+        merge(1, k)
+        dma("SA"[k % 2], "dO", T.yl[:, a:b], T.Lw[:, SH + a:SH + b], ["L%d" % k], [])
     wait("G", [(s, v) for s, v in count.items()])

@@ -6,20 +6,23 @@ SH = 32
 NL, NR = W + SH, W
 LW, RW = 1768, 1736
 BIG = 2048.0
-CH = W // 4
+WAVES = (0, 320, W)
+WIDTHS = ((80, 80, 80, 80), (160, 160, 320, 320))
+CALLS = ((0, (0, 1, 2, 3)), (1, (2, 3)), (1, (0, 1)))
+NW = len(WAVES) - 1
 WORLD = 256
 BANKS = ((0, 512), (512, 1024), (1024, W))
 
 SCRATCH = {
     "rti": ("sbuf", [128, W], "int32"), "rtu": ("sbuf", [128, W], "float16"),
-    "hop": ("sbuf", [128, CH], "float16"), "land": ("sbuf", [128, W], "float16"),
+    "land": ("sbuf", [128, W], "float16"),
     "lti": ("sbuf", [128, NL + 8], "int32"), "Lw": ("sbuf", [128, NL + 8], "float32"),
     "DL0": ("sbuf", [128, LW], "float32"), "DL1": ("sbuf", [128, LW], "float32"),
     "Rr": ("sbuf", [128, W + 8], "float32"), "Rw": ("sbuf", [128, RW], "float32"),
     "eui": ("sbuf", [128, 2 * K], "int32"), "evi": ("sbuf", [128, 2 * K], "int32"),
     "uo": ("sbuf", [128, 2 * K], "uint16"), "vo": ("sbuf", [128, 2 * K], "uint16"),
     "iw": ("sbuf", [128, NL], "float32"),
-    "nv": ("sbuf", [128, 2 * E], "float16"), "nu": ("sbuf", [128, E], "float16"),
+    "nv": ("sbuf", [128, 2 * E], "float16"), "nu": ("sbuf", [128, E], "float16"), "U16": ("sbuf", [128, W], "float16"),
     "xo": ("sbuf", [128, 6 * K], "uint16"), "so": ("sbuf", [128, 6 * K], "uint16"),
     "zz": ("sbuf", [128, 6 * K], "float32"), "mx": ("sbuf", [128, 6 * K], "float32"),
     "DU": ("sbuf", [128, NL], "float32"), "D16": ("sbuf", [128, W], "float16"), "L16": ("sbuf", [128, W], "float16"),
@@ -28,7 +31,7 @@ SCRATCH = {
     "yas": ("sbuf", [128, 2 * E], "float32"),
     "ji": ("sbuf", [128, 128], "int32"), "jg": ("sbuf", [128, 128], "int32"), "Tl": ("sbuf", [128, 128], "float16"),
     "O16": ("sbuf", [128, 128], "float16"), "nO16": ("sbuf", [128, 128], "float16"), "I16": ("sbuf", [128, 128], "float16"),
-    "nI16": ("sbuf", [128, 128], "float16"), "I2": ("sbuf", [128, 128], "float16"), "IB": ("sbuf", [128, 128], "float16"),
+    "nI16": ("sbuf", [128, 128], "float16"), "I2": ("sbuf", [128, 128], "float16"), "IU": ("sbuf", [128, 128], "float16"),
     "Mb": ("sbuf", [128, 128], "float16"), "MB": ("sbuf", [128, 128], "float16"),
     "B16": ("sbuf", [128, 144], "float16"), "KE": ("sbuf", [128, K], "float16"),
     "KL": ("sbuf", [128, E], "float16"), "KR": ("sbuf", [128, E], "float16"), "Yw": ("sbuf", [128, 8], "float16"),
@@ -51,8 +54,8 @@ for _t in range(2):
 for _n in ("PX0", "PX1", "PA", "PB", "PC", "PL0", "PL1", "PL2"):
     SCRATCH[_n] = ("psum", [128, 512], "float32")
 
-SEMAPHORES = ["sV", "sA", "sP", "sG", "hopin", "sent", "arr0", "arr1", "arr2", "arr3",
-              "dR0", "dR1", "dL", "dU", "dV", "dC", "dY0", "dY1", "dO"]
+SEMAPHORES = ["sV", "sA", "sP", "sG", "sent", "hop0", "hop1", "arr0", "arr1", "arr2", "arr3", "arr4",
+              "dR0", "dR1", "dR2", "dL", "dU", "dV", "dC", "dY0", "dY1", "dO"]
 
 
 def routes(T, topo):
@@ -76,6 +79,11 @@ def routes(T, topo):
     return out
 
 
+def piece(w, k):
+    a = WAVES[w] + sum(WIDTHS[w][:k])
+    return a, a + WIDTHS[w][k]
+
+
 def bits(engines):
     return sum(1 << e for e in engines)
 
@@ -86,10 +94,12 @@ def rank_program(g, core, T, topo):
         for s, c, d, k, eng in rts:
             if c == core:
                 rid, pid = topo.addr(d, core)
-                g.wait_ge(T.sem.hopin, len(eng))
-                g.remote_dma(T.land[:, k * CH:(k + 1) * CH], T.hop[:], T.sem["arr%d" % k], T.sem.sent, pid, rid,
-                             topo.mask(core, d))
-                g.wait_ge(T.sem.sent, len(topo.engines(core, d)))
+                for w in range(NW):
+                    a, b = piece(w, k)
+                    g.wait_ge(T.sem["hop%d" % w], len(eng))
+                    g.remote_dma(T.land[:, a:b], T.land[:, a:b], T.sem["arr%d" % (k + 1 if w else 0)], T.sem.sent,
+                                 pid, rid, topo.mask(core, d))
+                g.wait_ge(T.sem.sent, NW * len(topo.engines(core, d)))
         return
 
     Q = {"V": g.vector, "A": g.scalar, "P": g.tensor, "G": g, "S": g.sync}
@@ -166,8 +176,8 @@ def rank_program(g, core, T, topo):
     def act(out, in_, func, rd, wr, bias=0.0, scale=1.0):
         op("A", lambda: A.activation(out, in_, func, bias=bias, scale=scale), rd, wr)
 
-    def iota(out, step, n, cm, key):
-        op("G", lambda: g.iota(out, [[step, n]], 0, cm, allow_small_or_imprecise_dtypes=True), [], [key])
+    def iota(out, step, n, cm, key, base=0):
+        op("G", lambda: g.iota(out, [[step, n]], base, cm, allow_small_or_imprecise_dtypes=True), [], [key])
 
     def col(buf, i, a=0, b=K):
         return T[buf][:, i * K + a:i * K + b]
@@ -181,72 +191,79 @@ def rank_program(g, core, T, topo):
 
     NV = [(T.nv[:, t * E:(t + 1) * E], "nv%d" % t) for t in range(2)]
 
-    h = W // 2
-    dma("S", "dR0", T.rti[:, 0:h], T.rt[:, 0:h], [], ["rti0"])
-    dma("S", "dR1", T.rti[:, h:W], T.rt[:, h:W], [], ["rti1"])
+    for j, (w, ks) in enumerate(CALLS):
+        a, b = piece(w, ks[0])[0], piece(w, ks[-1])[1]
+        dma("S", "dR%d" % j, T.rti[:, a:b], T.rt[:, a:b], [], ["rti%d" % j])
     dma("S", "dU", T.eui[:], T.eu[:], [], ["eui"])
     dma("S", "dV", T.evi[:], T.ev[:], [], ["evi"])
     dma("S", "dL", T.lti[:, SH:NL], T.lt[:], [], ["lti"])
 
+    HW = NL // 2
     iota(T.pi[:], 0, 1, 1, "pi")
     iota(T.ji[:], 1, 128, 0, "ji")
     fill(T.nn[:], float(NL), "nn")
     act(T.Rr[:, W:W + 8], T.nn[:], ACT.Silu, ["nn"], ["Rrn"])
-    fill(T.B16[:], 0.0, "B16")
-    fill(T.KL[:], NR / 16.0, "KL")
-    fill(T.KR[:], NL / 16.0, "KR")
-    fill(T.lti[:, 0:SH], 0, "lti0")
-    fill(T.lti[:, NL:NL + 8], NR, "ltin")
-    fill(T.Lw[:, 0:SH], 0.0, "Lw0")
-    fill(T.Lw[:, NL:NL + 8], float(NR), "Lwn")
+    fill(T.DL0[:, 0:HW], 0.0, "DL0")
     ts(T.ci[:], T.pi[:], 15, None, ALU.bitwise_and, None, ["pi"], ["ci"])
     ts(T.gi[:], T.pi[:], 4, None, ALU.arith_shift_right, None, ["pi"], ["gi"])
     cp(T.pf[:], T.pi[:], ["pi"], ["pf"])
-    cp(T.cf[:], T.ci[:], ["ci"], ["cf"])
-    cp(T.gf[:], T.gi[:], ["gi"], ["gf"])
     ts(T.jg[:], T.ji[:], 4, None, ALU.arith_shift_right, None, ["ji"], ["jg"])
-    ts(T.I16[:], T.ji[:], T.pf[:], None, ALU.is_equal, None, ["ji", "pf"], ["I16"])
-    ts(T.O16[:], T.jg[:], T.gf[:], None, ALU.is_equal, None, ["jg", "gf"], ["O16"])
-    ts(T.Tl[:], T.ji[:], T.pf[:], -1.0, ALU.is_gt, ALU.mult, ["ji", "pf"], ["Tl"])
+    cp(T.gf[:], T.gi[:], ["gi"], ["gf"])
+    cp(T.cf[:], T.ci[:], ["ci"], ["cf"])
+    fill(T.B16[:], 0.0, "B16")
+    fill(T.lti[:, 0:SH], 0, "lti0")
+    fill(T.lti[:, NL:NL + 8], NR, "ltin")
+    iota(T.iw[:, 0:NL // 4], -1, NL // 4, 0, "iw", NL)
+    for n in (NL // 4, HW):
+        act(T.iw[:, n:2 * n], T.iw[:, 0:n], ACT.Identity, ["iw"], ["iw"], bias=-float(n))
+
+    def more_constants():
+        ts(T.Tl[:], T.ji[:], T.pf[:], -1.0, ALU.is_gt, ALU.mult, ["ji", "pf"], ["Tl"])
+        ts(T.O16[:], T.jg[:], T.gf[:], None, ALU.is_equal, None, ["jg", "gf"], ["O16"])
+        ts(T.I16[:], T.ji[:], T.pf[:], None, ALU.is_equal, None, ["ji", "pf"], ["I16"])
+        tt(T.Tl[:], T.Tl[:], T.O16[:], ALU.mult, ["Tl", "O16"], ["Tl"])
+
+    def last_constants():
+        tt(T.Mb[:], T.Tl[:], T.I16[:], ALU.add, ["Tl", "I16"], ["Mb"])
+        act(T.MB[:], T.Mb[:], ACT.Identity, ["Mb"], ["MB"], scale=BIG)
 
     mine = [r for r in rts if r[0] == core]
-    for half in range(2):
-        a, b, c_ = half * h, half * h + CH, (half + 1) * h
-        cp(T.rtu[:, a:b], T.rti[:, a:b], ["rti%d" % half], ["rtu%d" % (2 * half)])
-        act(T.rtu[:, b:c_], T.rti[:, b:c_], ACT.Identity, ["rti%d" % half], ["rtu%d" % (2 * half + 1)])
-        wait("G", [writer["rtu%d" % (2 * half)], writer["rtu%d" % (2 * half + 1)]])
+    for j, (w, ks) in enumerate(CALLS):
+        a, b = piece(w, ks[0])[0], piece(w, ks[-1])[1]
+        m = (a + b) // 2 if j else b
+        cp(T.rtu[:, a:m], T.rti[:, a:m], ["rti%d" % j], ["rtv%d" % j])
+        if j:
+            act(T.rtu[:, m:b], T.rti[:, m:b], ACT.Identity, ["rti%d" % j], ["rta%d" % j])
+        wait("G", [writer[x % j] for x in ("rtv%d", "rta%d") if x % j in writer])
         trs = []
-        for s, c, d, k, eng in mine[2 * half:2 * half + 2]:
-            rid, pid = topo.addr(c, core)
-            trs.append(RemoteDMATransfer(dst_ids=[DstId(rid=rid, pnc=pid)], dma_engine_mask=bits(eng), remote_sem=T.sem.hopin,
-                                         src=T.rtu[:, k * CH:(k + 1) * CH], dst=T.hop[:]))
-            count["sent"] = count.get("sent", 0) + len(eng)
+        for s, c, d, k, eng in mine:
+            if k in ks:
+                rid, pid = topo.addr(c, core)
+                a, b = piece(w, k)
+                trs.append(RemoteDMATransfer(dst_ids=[DstId(rid=rid, pnc=pid)], dma_engine_mask=bits(eng),
+                                             remote_sem=T.sem["hop%d" % w], src=T.rtu[:, a:b], dst=T.land[:, a:b]))
+                count["sent"] = count.get("sent", 0) + len(eng)
         g.remote_dma_fused(trs, local_sem=T.sem.sent)
-    iota(T.DL0[:, 0:NL], 0, NL, 0, "DL0")
+        if j == 0:
+            more_constants()
+    last_constants()
     iota(T.DU[:, SH:NL], 0, W, 0, "DU")
-    iota(T.DL1[:, SH:NL], 0, W, 0, "DL1")
 
-    act(T.iw[:, 0:128], T.ji[:], ACT.Identity, ["ji"], ["iw"], scale=-1.0)
-    n = 128
-    while n < NL:
-        m = min(n, NL - n)
-        act(T.iw[:, n:n + m], T.iw[:, 0:m], ACT.Identity, ["iw"], ["iw"], bias=-float(n))
-        n += m
-    tt(T.Tl[:], T.Tl[:], T.O16[:], ALU.mult, ["Tl", "O16"], ["Tl"])
-    ts(T.uo[:], T.eui[:], float(SH), None, ALU.add, None, ["eui"], ["uo"])
-    cp(T.vo[:], T.evi[:], ["evi"], ["vo"])
-    tt(T.Mb[:], T.Tl[:], T.I16[:], ALU.add, ["Tl", "I16"], ["Mb"])
-    ts(T.KE[:], T.ji[:, 0:K], 1.0 / 1024, None, ALU.mult, None, ["ji"], ["KE"])
-    ts(T.IB[:], T.I16[:], BIG, None, ALU.mult, None, ["I16"], ["IB"])
-    ts(T.MB[:], T.Mb[:], BIG, None, ALU.mult, None, ["Mb"], ["MB"])
-    ts(T.nO16[:], T.O16[:], -1.0, None, ALU.mult, None, ["O16"], ["nO16"])
-    ts(T.nI16[:], T.I16[:], -1.0, None, ALU.mult, None, ["I16"], ["nI16"])
-    ts(T.I2[:], T.I16[:], 2.0, None, ALU.mult, None, ["I16"], ["I2"])
+    fill(T.Lw[:, 0:SH], 0.0, "Lw0")
+    fill(T.Lw[:, NL:NL + 8], float(NR), "Lwn")
     ts(T.Yw[:], T.O16[:, 0:128:16], T.cf[:], None, ALU.mult, None, ["O16", "cf"], ["Yw"])
-    cp(T.B16[:, 15:143:16], T.O16[:, 0:128:16], ["O16", "B16"], ["B16"])
-    ts(T.bL[:], T.cf[:], float(K), float(NL + 1 - 1024 * NL), ALU.mult, ALU.add, ["cf"], ["bL"])
-    ts(T.bR[:], T.cf[:], float(K), float(NR + 1 - 1024 * NR), ALU.mult, ALU.add, ["cf"], ["bR"])
-    ts(T.bM[:], T.cf[:], -0.5, 0.5, ALU.mult, ALU.add, ["cf"], ["bM"])
+    cp(T.vo[:], T.evi[:], ["evi"], ["vo"])
+    ts(T.uo[:], T.eui[:], float(SH), None, ALU.add, None, ["eui"], ["uo"])
+    IW = ["iw"]
+    cp(NV[0][0], T.iw[:].indirect(col("vo", 0)), IW + ["vo"], ["nv0"])
+    act(NV[1][0], T.iw[:].indirect(col("vo", 1)), ACT.Identity, IW + ["vo"], ["nv1"])
+    cp(full("nu"), T.iw[:].indirect(col("uo", 0)), IW + ["uo"], ["nu"])
+    for name, src, by in (("nO16", "O16", -1.0), ("nI16", "I16", -1.0), ("I2", "I16", 2.0), ("IU", "I16", -1.0 / SH)):
+        act(T[name][:], T[src][:], ACT.Identity, [src], [name], scale=by)
+    act(T.KE[:], T.ji[:, 0:K], ACT.Identity, ["ji"], ["KE"], scale=1.0 / 1024)
+    act(T.B16[:, 15:143:16], T.O16[:, 0:128:16], ACT.Identity, ["O16", "B16"], ["B16"])
+    fill(T.KR[:], NL / 16.0, "KR")
+    fill(T.KL[:], NR / 16.0, "KL")
 
     LT = ["lti", "lti0", "ltin"]
     LN = ["L0", "L1", "L2", "Lw0", "Lwn"]
@@ -260,26 +277,14 @@ def rank_program(g, core, T, topo):
         d = "DL%d" % t
         ts(T[d][:].indirect(col("uo", t, a, b)), full("Xu", a, b), -1.0, 0.0, ALU.mult, ALU.add, ["uo", "Xu"], [d])
 
-    def change_u(t, bank, by=1.0):
-        lin(bank, [("I16", NV[t]), ("MB", "fu")])
-        act(full("Xu"), full(bank), ACT.Relu, [bank], ["Xu"], bias=(NR - BIG) * by, scale=by)
-
-    def narrow(k):
+    def narrow(dst, src, k, key=None):
         a, b = BANKS[k]
-        act(T.L16[:, a:b], T.Lw[:, SH + a:SH + b], ACT.Identity, ["L%d" % k], ["L16%d" % k])
+        op("G", lambda: g.affine_select(T[dst][:, a:b], T[src][:, SH + a:SH + b], [[0, b - a]], ALU.is_ge, 0.0, 0, 0),
+           [key or src], [dst + str(k)])
 
-    def narrow_u(k):
+    def hold(k, terms, start=True, stop=True):
         a, b = BANKS[k]
-        act(T.D16[:, a:b], T.DU[:, SH + a:SH + b], ACT.Identity, ["DU"], ["D16%d" % k], scale=-1.0 / SH)
-
-    def hold_sum(k):
-        a, b = BANKS[k]
-        mm("PL%d" % k, T["PL%d" % k][:, 0:b - a], [(T.I16[:], T.L16[:, a:b], ["I16", "L16%d" % k]),
-                                                   (T.I16[:], T.D16[:, a:b], ["I16", "D16%d" % k])])
-
-    def hold(k, src, keys):
-        a, b = BANKS[k]
-        act(T["PL%d" % k][:, 0:b - a], src[:, SH + a:SH + b], ACT.Identity, keys, ["PL%d" % k])
+        mm("PL%d" % k, T["PL%d" % k][:, 0:b - a], [(T[m][:], T[x][:, a:b], [m, x + str(k)]) for m, x in terms], start, stop)
 
     def merge(t, k, a=None, b=None):
         a0, b0 = BANKS[k]
@@ -287,33 +292,37 @@ def rank_program(g, core, T, topo):
         tt(T.Lw[:, SH + a:SH + b], T["DL%d" % t][:, SH + a:SH + b], T["PL%d" % k][:, a - a0:b - a0], ALU.add,
            ["DL%d" % t, "PL%d" % k], ["L%d" % k])
 
-    cp(NV[0][0], T.iw[:].indirect(col("vo", 0)), ["iw", "vo"], ["nv0"])
-    cp(T.nu[:], T.iw[:].indirect(col("uo", 0)), ["iw", "uo"], ["nu"])
-    act(full("fu"), T.lti[:].indirect(col("uo", 0)), ACT.Relu, LT + ["uo"], ["fu"], bias=-float(NR - 1))
-    cp(NV[1][0], T.iw[:].indirect(col("vo", 1)), ["iw", "vo"], ["nv1"])
-    ts(full("Wu"), T.lti[:].indirect(col("uo", 1)), -1.0, float(NR), ALU.mult, ALU.add, LT + ["uo"], ["Wu"])
-    change_u(0, "PA")
+    lin("PA", [("I16", NV[0])], stop=False); lin("PC", [("I16", "nu")], stop=False)
+    ts(full("fu"), T.lti[:].indirect(col("uo", 0)), float(NR), None, ALU.is_equal, None, LT + ["uo"], ["fu"])
+    act(full("Wu"), T.lti[:].indirect(col("uo", 1)), ACT.Identity, LT + ["uo"], ["Wu"], scale=-1.0, bias=float(NR))
+    lin("PA", [("MB", "fu")], start=False)
+    act(full("Xu"), full("PA"), ACT.Relu, ["PA"], ["Xu"], bias=NR - NL - BIG)
     lin("PB", [("Mb", "fu")])
     act(full("ma0"), full("PB"), ACT.Relu, ["PB"], ["ma0"])
-    lin("PC", [("I16", "nu"), ("MB", "fu")])
-    scatter_u(0)
-    act(full("Zu"), full("PC"), ACT.Relu, ["PC"], ["Zu"], bias=float(NL) - BIG)
-    colours(0, "PB")
+    lin("PC", [("MB", "fu")], start=False)
+    fill(T.DL0[:, HW:NL], 0.0, "DL0b")
+    ts(T.bL[:], T.cf[:], float(K), float(NL + 1 - 1024 * NL), ALU.mult, ALU.add, ["cf"], ["bL"])
+    ts(T.bR[:], T.cf[:], float(K), float(NR + 1 - 1024 * NR), ALU.mult, ALU.add, ["cf"], ["bR"])
+    ts(T.bM[:], T.cf[:], -0.5, 0.5, ALU.mult, ALU.add, ["cf"], ["bM"])
+    wait("V", [writer["DL0b"]])
+    scatter_u(0, 0, 16)
     for k in range(3):
-        hold(k, T.lti, ["lti"])
-    lin("PA", [("O16", "KR"), ("nI16", "Zu")], stop=False)
+        narrow("L16", "lti", k)
+    iota(T.DL1[:, SH:NL], 0, W, 0, "DL1")
+    lin("PA", [("O16", "KR")], stop=False)
 
-    for k in range(4):
-        r = [x for x in rts if x[2] == core and x[3] == k][0]
-        n = len(topo.engines(r[1], core))
-        count["arr%d" % k] = n
-        writer["land%d" % k] = ("arr%d" % k, n)
-        src, dst = T.land[:, k * CH:(k + 1) * CH], T.Rr[:, k * CH:(k + 1) * CH]
-        if k % 2 == 0:
-            ts(dst, src, float(SH), None, ALU.add, None, ["land%d" % k], ["Rr%d" % k])
+    RR = ["Rrn"]
+    come = [len(topo.engines(r[1], core)) for r in rts if r[2] == core]
+    for w, n in enumerate([sum(come)] + come):
+        count["arr%d" % w] = n
+        writer["land%d" % w] = ("arr%d" % w, n)
+    for e, (a, b), w in (("A", WAVES[0:2], 0), ("A", piece(1, 0), 1), ("V", piece(1, 1), 2), ("A", piece(1, 2), 3), ("V", piece(1, 3), 4)):
+        key = "R%s%d" % (e, w)
+        if e == "V":
+            ts(T.Rr[:, a:b], T.land[:, a:b], float(SH), None, ALU.add, None, ["land%d" % w], [key])
         else:
-            act(dst, src, ACT.Identity, ["land%d" % k], ["Rr%d" % k], bias=float(SH))
-    RR = ["Rr0", "Rr1", "Rr2", "Rr3", "Rrn"]
+            act(T.Rr[:, a:b], T.land[:, a:b], ACT.Identity, ["land%d" % w], [key], bias=float(SH))
+        RR.append(key)
     dma("S", "dC", T.Rw[:, 0:W + 8], T.Rr[:], RR, ["R"])
 
     def table(t, i):
@@ -353,8 +362,9 @@ def rank_program(g, core, T, topo):
     def spare(i):
         tt(col("mx", i), T[bank(i)][:, 0:K], col("zz", i), ALU.max, [bank(i), "zz%d" % i], ["mx%d" % i])
 
-    def spare2(i):
-        cp(col("so", i), col("mx", i), ["mx%d" % i], ["so%d" % i])
+    def spare2(i, n=1):
+        cp(col("so", i, 0, n * K), col("mx", i, 0, n * K), ["mx%d" % j for j in range(i, i + n)],
+           ["so%d" % j for j in range(i, i + n)])
 
     def column(t, i, e="A"):
         win, keys = table(t, i)
@@ -365,7 +375,7 @@ def rank_program(g, core, T, topo):
             cp(full("G%d" % i), win.indirect(o), keys + [ok], ["G%d" % i])
 
     def out(i, b):
-        act(full("N%d" % i), full(b), ACT.Identity, [b], ["N%d" % i])
+        act(full("N%d" % i), full(b), ACT.Identity, [b], ["N%d" % i], bias=-float(NL) if i == 1 else 0.0)
 
     def scatter_left(t, i, a=0, b=K):
         d = "DL%d" % t
@@ -382,60 +392,66 @@ def rank_program(g, core, T, topo):
         o, ok = (col("vo", 0), "vo") if i == 0 else (col("so", i), "so%d" % i)
         op("A", lambda: A.activation(T.Rw[:].indirect(o), full("N%d" % i), ACT.Silu), [ok, "N%d" % i], ["R"])
 
+    def begin(b, m, x):
+        lin(b, [(m, x)], stop=False)
+
+    def end(b, *terms):
+        lin(b, list(terms), start=False)
+
     def signs(t, b):
         lin(b, [("I2", "ma%d" % t), ("nI16", "mb%d" % t)])
         act(full("sg%d" % t), full(b), ACT.Sign, [b], ["sg%d" % t])
 
     step(0, 0)
     act(full("sv"), T.Rr[:].indirect(col("vo", 0)), ACT.Sign, RR + ["vo"], ["sv"], bias=0.5 - NL)
+    act(full("Zu"), full("PC"), ACT.Relu, ["PC"], ["Zu"], bias=-BIG)
     lin("PB", [("Mb", "sv")]); spread(0)
     act(full("mb0"), full("PB"), ACT.Relu, ["PB", "bM"], ["mb0"], bias=T.bM[:], scale=0.5)
-    column(0, 0, "V"); take(1); step(0, 1); ended(1); signs(0, "PC"); lin("PA", [("nO16", "H0")], start=False)
-    lin("PB", [("I16", NV[0])], stop=False); spread(1); spare(1); lin("PB", [("O16", "H1")], start=False)
-    change_right(0, "PA"); spare2(1); new_right(0, "PC")
-    take(2); step(0, 2); ended(2); out(1, "PB"); out(0, "PC"); column(0, 2); scatter_right(0)
-    lin("PA", [("O16", "H0")], stop=False); spare(2); spread(2); lin("PA", [("nO16", "H2")], start=False)
-    scatter_left(0, 1, 0, 12); spare2(2)
-    take(3); ended(3, "V"); step(0, 3); spare(3); change_right(2, "PA")
-    lin("PB", [("nO16", "H1")], stop=False); spread(3); new_right(2, "PC"); lin("PB", [("O16", "H3")], start=False)
-    spare2(3); scatter_left(0, 1, 12, 18)
-    take(4); ended(4, "V"); step(0, 4)
-    out(2, "PC"); out(3, "PB"); column(0, 4); scatter_right(2)
-    lin("PA", [("O16", "H2")], stop=False); spare(4); lin("PA", [("nO16", "H4")], start=False); spread(4)
-    lin("PB", [("O16", "KL"), ("nO16", "H3")])
-    spare2(4); change_right(4, "PA"); new_right(4, "PC"); scatter_left(0, 1, 18, K)
-    ended(5, "V"); out(5, "PB"); out(4, "PC"); scatter_right(4)
-    scatter_left(0, 3, 0, 14); spare(5); scatter_left(0, 3, 14, K); spare2(5); scatter_left(0, 5)
+    scatter_u(0, 16, K)
+    take(1); step(0, 1); ended(1); signs(0, "PC"); end("PA", ("nO16", "H0"), ("nI16", "Zu"))
+    spare(1); change_right(0, "PA"); spread(1); lin("PB", [("I16", NV[0]), ("O16", "H1")]); column(0, 0)
+    take(2); ended(2); new_right(0, "PC"); step(0, 2); out(1, "PB"); spare(2); spare2(1, 2)
+    spread(2); lin("PA", [("O16", "H0"), ("nO16", "H2")]); scatter_left(0, 1, 0, 12)
+    take(3); step(0, 3); begin("PB", "nO16", "H1"); out(0, "PC"); column(0, 2); scatter_right(0); scatter_left(0, 1, 12, 18)
+    begin("PC", "I16", "G2"); change_right(2, "PA"); spread(3); ended(3); end("PB", ("O16", "H3"))
+    take(4); begin("PA", "O16", "H2"); scatter_left(0, 1, 18, 22); end("PC", ("I16", "E2")); step(0, 4)
+    ended(4); out(3, "PB"); spare(3); end("PA", ("nO16", "H4")); spare(4); out(2, "PC")
+    scatter_left(0, 1, 22, K); spare2(3, 2); begin("PB", "O16", "KL"); change_right(4, "PA"); column(0, 4)
+    scatter_left(0, 3); spread(4); scatter_right(2); new_right(4, "PC"); ended(5); end("PB", ("nO16", "H3"))
+    spare(5); tt(full("N5"), full("PB"), full("sg0"), ALU.mult, ["PB", "sg0"], ["N5"]); out(4, "PC"); spare2(5); scatter_right(4)
+    cp(T.DL0[:].indirect(col("so", 5)), full("N5"), ["so5", "N5"], ["DL0"])
 
+    begin("PX0", "I16", NV[1])
+    for k in range(3):
+        hold(k, [("I16", "L16")])
     column(1, 0)
-    lin("PC", [("I16", NV[1])], stop=False)
-    lin("PA", [("I16", "G0")], stop=False)
     tt(full("fu"), T.DL0[:, 0:NL].indirect(col("uo", 1)), full("Wu"), ALU.is_equal, ["DL0", "uo", "Wu"], ["fu"])
     ts(full("sv"), full("G0"), float(NL), None, ALU.is_equal, None, ["G0"], ["sv"])
-    lin("PA", [("MB", "fu")], start=False)
+    lin("PA", [("I16", "G0"), ("MB", "fu")])
     act(full("H0"), full("PA"), ACT.Relu, ["PA"], ["H0"], bias=-BIG)
-    lin("PB", [("Mb", "sv")])
+    lin("PB", [("Mb", "sv")]); end("PX0", ("MB", "fu")); spread(0)
     act(full("mb1"), full("PB"), ACT.Relu, ["PB"], ["mb1"])
-    lin("PC", [("MB", "fu")], start=False)
-    act(full("Xu"), full("PC"), ACT.Relu, ["PC"], ["Xu"], bias=(NR - BIG) * SH, scale=float(SH))
-    spread(0)
-    merge(0, 0); merge(0, 1); merge(0, 2)
+    act(full("Xu"), full("PX0"), ACT.Relu, ["PX0"], ["Xu"], bias=(NR - NL - BIG) * SH, scale=float(SH))
+    merge(0, 0); merge(0, 2); merge(0, 1)
+    for k in (0, 2, 1):
+        narrow("L16", "Lw", k, "L%d" % k)
     ts(full("ma1"), full("H0"), 0.0, None, ALU.is_gt, None, ["H0"], ["ma1"])
-    take(1); ended(1, "V"); step(1, 1); signs(1, "PB")
-    lin("PA", [("I16", NV[1])], stop=False); spare(1); spread(1, True); lin("PA", [("O16", "H1")], start=False)
-    narrow(0); narrow(2); out(1, "PA"); spare2(1)
-    take(2); step(1, 2); spread(2)
+    take(1); ended(1); begin("PA", "I16", NV[1]); step(1, 1); signs(1, "PC"); spare(1); spare2(1)
+    spread(1); end("PA", ("O16", "H1")); out(1, "PA")
+    take(2); step(1, 2); spread(2); scatter_left(1, 1, 0, 12); begin("PA", "nO16", "H1")
     op("A", lambda: A.activation(T.DU[:].indirect(col("uo", 1)), full("Xu"), ACT.Silu), ["uo", "Xu"], ["DU"])
-    scatter_left(1, 1, 0, 14)
-    take(3); ended(3, "V"); step(1, 3); narrow(1); narrow_u(0)
-    lin("PA", [("nO16", "H1")], stop=False); lin("PB", [("O16", "KL")], stop=False); spare(3); spread(3, True)
-    lin("PA", [("O16", "H3")], start=False); lin("PB", [("nO16", "H3")], start=False); out(3, "PA"); out(5, "PB")
-    scatter_left(1, 1, 14, K); spare2(3)
-    take(4); step(1, 4); narrow_u(1); narrow_u(2); hold_sum(0); spread(4)
-    scatter_left(1, 3, 0, 14); ended(5); hold_sum(1); hold_sum(2); colours(1, "PC")
-    scatter_left(1, 3, 14, 20); spare(5); scatter_left(1, 3, 20, K); spare2(5); scatter_left(1, 5)
-    for k in range(3):
+    for k in (2, 0, 1):
+        narrow("U16", "DU", k)
+    take(3); step(1, 3); ended(3, "V"); hold(0, [("I16", "L16")], stop=False); hold(2, [("I16", "L16")], stop=False)
+    spread(3); scatter_left(1, 1, 12, 24); spare(3); scatter_left(1, 1, 24, K); end("PA", ("O16", "H3")); out(3, "PA")
+    take(4); lin("PB", [("nO16", "H3")]); spare2(3); step(1, 4); colours(1, "PC"); spread(4); ended(5)
+    act(full("N5"), full("PB"), ACT.Identity, ["PB"], ["N5"], bias=float(NR))
+    colours(0, "PC"); hold(1, [("I16", "L16")], stop=False)
+    for k in (2, 0, 1):
+        hold(k, [("IU", "U16")], start=False)
+    scatter_left(1, 3, 0, 20); spare(5); scatter_left(1, 3, 20, K); spare2(5); scatter_left(1, 5)
+    for j, k in enumerate((2, 0, 1)):
         a, b = BANKS[k]
         merge(1, k)
-        dma("SA"[k % 2], "dO", T.yl[:, a:b], T.Lw[:, SH + a:SH + b], ["L%d" % k], [])
+        dma("SA"[j % 2], "dO", T.yl[:, a:b], T.Lw[:, SH + a:SH + b], ["L%d" % k], [])
     wait("G", [(s, v) for s, v in count.items()])

from concourse.bass import DstId, RemoteDMATransfer
from concourse.mybir import AluOpType as ALU, ActivationFunctionType as ACT

W, E, K = 1280, 448, 28
SH = 32
NL, NR = W + SH, W
LW, RW = 1768, 1736
BIG = 2048.0
WAVES = (0, 320, W)
WIDTHS = ((80, 80, 80, 80), (160, 160, 320, 320))
CALLS = ((0, (0, 1, 2, 3)), (1, (2, 3)), (1, (0, 1)))
NW = len(WAVES) - 1
WORLD = 256
BANKS = ((0, 512), (512, 1024), (1024, W))

SCRATCH = {
    "rti": ("sbuf", [128, W], "int32"), "rtu": ("sbuf", [128, W], "float16"),
    "land": ("sbuf", [128, W], "float16"),
    "lti": ("sbuf", [128, NL + 8], "int32"), "Lw": ("sbuf", [128, NL + 8], "float32"),
    "DL0": ("sbuf", [128, LW], "float32"), "DL1": ("sbuf", [128, LW], "float32"),
    "Rr": ("sbuf", [128, W + 8], "float32"), "Rw": ("sbuf", [128, RW], "float32"),
    "eui": ("sbuf", [128, 2 * K], "int32"), "evi": ("sbuf", [128, 2 * K], "int32"),
    "uo": ("sbuf", [128, 2 * K], "uint16"), "vo": ("sbuf", [128, 2 * K], "uint16"),
    "iw": ("sbuf", [128, NL], "float32"),
    "nv": ("sbuf", [128, 2 * E], "float16"), "nu": ("sbuf", [128, E], "float16"), "U16": ("sbuf", [128, W], "float16"),
    "xo": ("sbuf", [128, 6 * K], "uint16"), "so": ("sbuf", [128, 6 * K], "uint16"),
    "zz": ("sbuf", [128, 6 * K], "float32"), "mx": ("sbuf", [128, 6 * K], "float32"),
    "DU": ("sbuf", [128, NL], "float32"), "D16": ("sbuf", [128, W], "float16"), "L16": ("sbuf", [128, W], "float16"),
    "Wu": ("sbuf", [128, E], "float32"), "Xu": ("sbuf", [128, E], "float32"), "Zu": ("sbuf", [128, E], "float16"),
    "fu": ("sbuf", [128, E], "bfloat16"), "sv": ("sbuf", [128, E], "bfloat16"),
    "yas": ("sbuf", [128, 2 * E], "float32"),
    "ji": ("sbuf", [128, 128], "int32"), "jg": ("sbuf", [128, 128], "int32"), "Tl": ("sbuf", [128, 128], "float16"),
    "O16": ("sbuf", [128, 128], "float16"), "nO16": ("sbuf", [128, 128], "float16"), "I16": ("sbuf", [128, 128], "float16"),
    "nI16": ("sbuf", [128, 128], "float16"), "I2": ("sbuf", [128, 128], "float16"), "IU": ("sbuf", [128, 128], "float16"),
    "Mb": ("sbuf", [128, 128], "float16"), "MB": ("sbuf", [128, 128], "float16"),
    "B16": ("sbuf", [128, 144], "float16"), "KE": ("sbuf", [128, K], "float16"),
    "KL": ("sbuf", [128, E], "float16"), "KR": ("sbuf", [128, E], "float16"), "Yw": ("sbuf", [128, 8], "float16"),
    "pi": ("sbuf", [128, 1], "int32"), "ci": ("sbuf", [128, 1], "int32"), "gi": ("sbuf", [128, 1], "int32"),
    "cf": ("sbuf", [128, 1], "float32"), "pf": ("sbuf", [128, 1], "float32"), "gf": ("sbuf", [128, 1], "float32"),
    "bL": ("sbuf", [128, 1], "float32"), "bR": ("sbuf", [128, 1], "float32"), "bM": ("sbuf", [128, 1], "float32"),
    "nn": ("sbuf", [128, 8], "float32"),
}
for _i in range(5):
    SCRATCH["H%d" % _i] = ("sbuf", [128, E], "float16")
for _i in (0, 2, 4):
    SCRATCH["G%d" % _i] = ("sbuf", [128, E], "float16")
    SCRATCH["E%d" % _i] = ("sbuf", [128, E], "float16")
for _i in range(6):
    SCRATCH["N%d" % _i] = ("sbuf", [128, E], "float32")
for _t in range(2):
    SCRATCH["ma%d" % _t] = ("sbuf", [128, E], "float16")
    SCRATCH["mb%d" % _t] = ("sbuf", [128, E], "float16")
    SCRATCH["sg%d" % _t] = ("sbuf", [128, E], "float32")
for _n in ("PX0", "PX1", "PA", "PB", "PC", "PL0", "PL1", "PL2"):
    SCRATCH[_n] = ("psum", [128, 512], "float32")

SEMAPHORES = ["sV", "sA", "sP", "sG", "sent", "hop0", "hop1", "arr0", "arr1", "arr2", "arr3", "arr4",
              "dR0", "dR1", "dR2", "dL", "dU", "dV", "dC", "dY0", "dY1", "dO"]


def routes(T, topo):
    out = []
    n = len(T.cores)
    for q in range(n):
        s, d = T.cores[q], T.cores[(q - 1) % n]
        far, near = {}, {}
        for c in range(WORLD):
            if T.rank_of(c) is None and topo.mates(c, d) and topo.may_write(s, c) and topo.may_write(c, d):
                far.setdefault(topo.die(c), c)
        for c in topo.cores_of(s):
            if T.rank_of(c) is None and topo.may_write(c, d):
                near.setdefault(topo.die(c), c)
        far, near = [far[k] for k in sorted(far)], [near[k] for k in sorted(near)]
        off = topo.engines(s, far[0])
        on = [e for e in topo.engines(s, near[0]) if e not in off]
        for k, (c, eng) in enumerate(((far[0], off[:len(off) // 2]), (far[1], off[len(off) // 2:]),
                                      (near[0], on[:len(on) // 2]), (near[1], on[len(on) // 2:]))):
            out.append((s, c, d, k, eng))
    return out


def piece(w, k):
    a = WAVES[w] + sum(WIDTHS[w][:k])
    return a, a + WIDTHS[w][k]


def bits(engines):
    return sum(1 << e for e in engines)


def rank_program(g, core, T, topo):
    rts = routes(T, topo)
    if T.rank_of(core) is None:
        for s, c, d, k, eng in rts:
            if c == core:
                rid, pid = topo.addr(d, core)
                for w in range(NW):
                    a, b = piece(w, k)
                    g.wait_ge(T.sem["hop%d" % w], len(eng))
                    g.remote_dma(T.land[:, a:b], T.land[:, a:b], T.sem["arr%d" % (k + 1 if w else 0)], T.sem.sent,
                                 pid, rid, topo.mask(core, d))
                g.wait_ge(T.sem.sent, NW * len(topo.engines(core, d)))
        return

    Q = {"V": g.vector, "A": g.scalar, "P": g.tensor, "G": g, "S": g.sync}
    own = {"V": "sV", "A": "sA", "P": "sP", "G": "sG"}
    known = {e: {} for e in Q}
    count, clock, writer, readers = {}, {}, {}, {}

    def wait(e, evs):
        need = {}
        for s, v in evs:
            if not (e == "P" and s == "sP") and known[e].get(s, 0) < v:
                need[s] = max(need.get(s, 0), v)
        for s in sorted(need, key=lambda x: x == own.get(e)):
            v = need[s]
            if known[e].get(s, 0) < v:
                Q[e].wait_ge(T.sem[s], v)
                for s2, v2 in clock.get((s, v), {s: v}).items():
                    known[e][s2] = max(known[e].get(s2, 0), v2)

    def deps(rd, wr):
        evs = [writer[k] for k in rd if k in writer]
        for k in wr:
            evs += readers.get(k, [])
            if k in writer:
                evs.append(writer[k])
        return evs

    def done(e, ins, rd, wr, sem, n):
        count[sem] = count.get(sem, 0) + n
        ins.then_inc(T.sem[sem], n)
        ev = (sem, count[sem])
        clock[ev] = dict(known[e])
        clock[ev][sem] = count[sem]
        for k in rd:
            readers.setdefault(k, []).append(ev)
        for k in wr:
            writer[k] = ev
            readers[k] = []

    def op(e, fn, rd, wr):
        wr = wr + [k for k in rd if k[0] == "P"]
        wait(e, deps(rd, wr))
        done(e, fn(), rd, wr, own[e], 1)

    def dma(e, sem, out, in_, rd, wr):
        wait(e, deps(rd, wr))
        done(e, Q[e].dma_start(out, in_), rd, wr, sem, 16)

    def mm(bank, out, terms, start=True, stop=True):
        rd = []
        for j, (lhsT, rhs, keys) in enumerate(terms):
            wait("P", deps(keys, [bank]))
            ins = g.tensor.matmul(out, lhsT, rhs, start and j == 0, stop and j == len(terms) - 1)
            rd += keys
        done("P", ins, rd, [bank], "sP", 1)

    V, A = g.vector, g.scalar

    def ts(out, in0, s1, s2, op0, op1, rd, wr):
        if s2 is None:
            op("V", lambda: V.tensor_scalar(out, in0, s1, None, op0), rd, wr)
        else:
            op("V", lambda: V.tensor_scalar(out, in0, s1, s2, op0, op1), rd, wr)

    def tt(out, in0, in1, alu, rd, wr):
        op("V", lambda: V.tensor_tensor(out, in0, in1, alu), rd, wr)

    def cp(out, in_, rd, wr):
        op("V", lambda: V.tensor_copy(out, in_), rd, wr)

    def fill(ap, val, key):
        op("V", lambda: V.memset(ap, val), [], [key])

    def act(out, in_, func, rd, wr, bias=0.0, scale=1.0):
        op("A", lambda: A.activation(out, in_, func, bias=bias, scale=scale), rd, wr)

    def iota(out, step, n, cm, key, base=0):
        op("G", lambda: g.iota(out, [[step, n]], base, cm, allow_small_or_imprecise_dtypes=True), [], [key])

    def col(buf, i, a=0, b=K):
        return T[buf][:, i * K + a:i * K + b]

    def full(name, a=0, b=K):
        return T[name][:, 16 * a:16 * b]

    def lin(bank, terms, start=True, stop=True):
        mm(bank, full(bank), [(T[m][:], full(x) if isinstance(x, str) else x[0], [m, x if isinstance(x, str) else x[1]])
                              for m, x in terms], start, stop)

    NV = [(T.nv[:, t * E:(t + 1) * E], "nv%d" % t) for t in range(2)]

    for j, (w, ks) in enumerate(CALLS):
        a, b = piece(w, ks[0])[0], piece(w, ks[-1])[1]
        dma("S", "dR%d" % j, T.rti[:, a:b], T.rt[:, a:b], [], ["rti%d" % j])
    dma("S", "dU", T.eui[:], T.eu[:], [], ["eui"])
    dma("S", "dV", T.evi[:], T.ev[:], [], ["evi"])
    dma("S", "dL", T.lti[:, SH:NL], T.lt[:], [], ["lti"])

    HW = NL // 2
    iota(T.pi[:], 0, 1, 1, "pi")
    iota(T.ji[:], 1, 128, 0, "ji")
    fill(T.nn[:], float(NL), "nn")
    act(T.Rr[:, W:W + 8], T.nn[:], ACT.Silu, ["nn"], ["Rrn"])
    fill(T.DL0[:, 0:HW], 0.0, "DL0")
    ts(T.ci[:], T.pi[:], 15, None, ALU.bitwise_and, None, ["pi"], ["ci"])
    ts(T.gi[:], T.pi[:], 4, None, ALU.arith_shift_right, None, ["pi"], ["gi"])
    cp(T.pf[:], T.pi[:], ["pi"], ["pf"])
    ts(T.jg[:], T.ji[:], 4, None, ALU.arith_shift_right, None, ["ji"], ["jg"])
    cp(T.gf[:], T.gi[:], ["gi"], ["gf"])
    cp(T.cf[:], T.ci[:], ["ci"], ["cf"])
    fill(T.B16[:], 0.0, "B16")
    fill(T.lti[:, 0:SH], 0, "lti0")
    fill(T.lti[:, NL:NL + 8], NR, "ltin")
    iota(T.iw[:, 0:NL // 4], -1, NL // 4, 0, "iw", NL)
    for n in (NL // 4, HW):
        act(T.iw[:, n:2 * n], T.iw[:, 0:n], ACT.Identity, ["iw"], ["iw"], bias=-float(n))

    def more_constants():
        ts(T.Tl[:], T.ji[:], T.pf[:], -1.0, ALU.is_gt, ALU.mult, ["ji", "pf"], ["Tl"])
        ts(T.O16[:], T.jg[:], T.gf[:], None, ALU.is_equal, None, ["jg", "gf"], ["O16"])
        ts(T.I16[:], T.ji[:], T.pf[:], None, ALU.is_equal, None, ["ji", "pf"], ["I16"])
        tt(T.Tl[:], T.Tl[:], T.O16[:], ALU.mult, ["Tl", "O16"], ["Tl"])

    def last_constants():
        tt(T.Mb[:], T.Tl[:], T.I16[:], ALU.add, ["Tl", "I16"], ["Mb"])
        act(T.MB[:], T.Mb[:], ACT.Identity, ["Mb"], ["MB"], scale=BIG)

    mine = [r for r in rts if r[0] == core]
    for j, (w, ks) in enumerate(CALLS):
        a, b = piece(w, ks[0])[0], piece(w, ks[-1])[1]
        m = (a + b) // 2 if j else b
        cp(T.rtu[:, a:m], T.rti[:, a:m], ["rti%d" % j], ["rtv%d" % j])
        if j:
            act(T.rtu[:, m:b], T.rti[:, m:b], ACT.Identity, ["rti%d" % j], ["rta%d" % j])
        wait("G", [writer[x % j] for x in ("rtv%d", "rta%d") if x % j in writer])
        trs = []
        for s, c, d, k, eng in mine:
            if k in ks:
                rid, pid = topo.addr(c, core)
                a, b = piece(w, k)
                trs.append(RemoteDMATransfer(dst_ids=[DstId(rid=rid, pnc=pid)], dma_engine_mask=bits(eng),
                                             remote_sem=T.sem["hop%d" % w], src=T.rtu[:, a:b], dst=T.land[:, a:b]))
                count["sent"] = count.get("sent", 0) + len(eng)
        g.remote_dma_fused(trs, local_sem=T.sem.sent)
        if j == 0:
            more_constants()
    last_constants()
    iota(T.DU[:, SH:NL], 0, W, 0, "DU")

    fill(T.Lw[:, 0:SH], 0.0, "Lw0")
    fill(T.Lw[:, NL:NL + 8], float(NR), "Lwn")
    ts(T.Yw[:], T.O16[:, 0:128:16], T.cf[:], None, ALU.mult, None, ["O16", "cf"], ["Yw"])
    cp(T.vo[:], T.evi[:], ["evi"], ["vo"])
    ts(T.uo[:], T.eui[:], float(SH), None, ALU.add, None, ["eui"], ["uo"])
    IW = ["iw"]
    cp(NV[0][0], T.iw[:].indirect(col("vo", 0)), IW + ["vo"], ["nv0"])
    act(NV[1][0], T.iw[:].indirect(col("vo", 1)), ACT.Identity, IW + ["vo"], ["nv1"])
    cp(full("nu"), T.iw[:].indirect(col("uo", 0)), IW + ["uo"], ["nu"])
    for name, src, by in (("nO16", "O16", -1.0), ("nI16", "I16", -1.0), ("I2", "I16", 2.0), ("IU", "I16", -1.0 / SH)):
        act(T[name][:], T[src][:], ACT.Identity, [src], [name], scale=by)
    act(T.KE[:], T.ji[:, 0:K], ACT.Identity, ["ji"], ["KE"], scale=1.0 / 1024)
    act(T.B16[:, 15:143:16], T.O16[:, 0:128:16], ACT.Identity, ["O16", "B16"], ["B16"])
    fill(T.KR[:], NL / 16.0, "KR")
    fill(T.KL[:], NR / 16.0, "KL")

    LT = ["lti", "lti0", "ltin"]
    LN = ["L0", "L1", "L2", "Lw0", "Lwn"]

    def colours(t, bank):
        mm(bank, T[bank][0:8, 0:E], [(T.Yw[:], full("ma%d" % t), ["Yw", "ma%d" % t])])
        act(T.yas[0:8, t * E:(t + 1) * E], T[bank][0:8, 0:E], ACT.Copy, [bank], ["yas%d" % t])
        dma("S", "dY%d" % t, T.ya[:, t * E:(t + 1) * E], T.yas[0:8, t * E:(t + 1) * E], ["yas%d" % t], [])

    def scatter_u(t, a=0, b=K):
        d = "DL%d" % t
        ts(T[d][:].indirect(col("uo", t, a, b)), full("Xu", a, b), -1.0, 0.0, ALU.mult, ALU.add, ["uo", "Xu"], [d])

    def narrow(dst, src, k, key=None):
        a, b = BANKS[k]
        op("G", lambda: g.affine_select(T[dst][:, a:b], T[src][:, SH + a:SH + b], [[0, b - a]], ALU.is_ge, 0.0, 0, 0),
           [key or src], [dst + str(k)])

    def hold(k, terms, start=True, stop=True):
        a, b = BANKS[k]
        mm("PL%d" % k, T["PL%d" % k][:, 0:b - a], [(T[m][:], T[x][:, a:b], [m, x + str(k)]) for m, x in terms], start, stop)

    def merge(t, k, a=None, b=None):
        a0, b0 = BANKS[k]
        a, b = (a0, b0) if a is None else (a, b)
        tt(T.Lw[:, SH + a:SH + b], T["DL%d" % t][:, SH + a:SH + b], T["PL%d" % k][:, a - a0:b - a0], ALU.add,
           ["DL%d" % t, "PL%d" % k], ["L%d" % k])

    lin("PA", [("I16", NV[0])], stop=False); lin("PC", [("I16", "nu")], stop=False)
    ts(full("fu"), T.lti[:].indirect(col("uo", 0)), float(NR), None, ALU.is_equal, None, LT + ["uo"], ["fu"])
    act(full("Wu"), T.lti[:].indirect(col("uo", 1)), ACT.Identity, LT + ["uo"], ["Wu"], scale=-1.0, bias=float(NR))
    lin("PA", [("MB", "fu")], start=False)
    act(full("Xu"), full("PA"), ACT.Relu, ["PA"], ["Xu"], bias=NR - NL - BIG)
    lin("PB", [("Mb", "fu")])
    act(full("ma0"), full("PB"), ACT.Relu, ["PB"], ["ma0"])
    lin("PC", [("MB", "fu")], start=False)
    fill(T.DL0[:, HW:NL], 0.0, "DL0b")
    ts(T.bL[:], T.cf[:], float(K), float(NL + 1 - 1024 * NL), ALU.mult, ALU.add, ["cf"], ["bL"])
    ts(T.bR[:], T.cf[:], float(K), float(NR + 1 - 1024 * NR), ALU.mult, ALU.add, ["cf"], ["bR"])
    ts(T.bM[:], T.cf[:], -0.5, 0.5, ALU.mult, ALU.add, ["cf"], ["bM"])
    wait("V", [writer["DL0b"]])
    scatter_u(0, 0, 16)
    for k in range(3):
        narrow("L16", "lti", k)
    iota(T.DL1[:, SH:NL], 0, W, 0, "DL1")
    lin("PA", [("O16", "KR")], stop=False)

    RR = ["Rrn"]
    come = [len(topo.engines(r[1], core)) for r in rts if r[2] == core]
    for w, n in enumerate([sum(come)] + come):
        count["arr%d" % w] = n
        writer["land%d" % w] = ("arr%d" % w, n)
    for e, (a, b), w in (("A", WAVES[0:2], 0), ("A", piece(1, 0), 1), ("V", piece(1, 1), 2), ("A", piece(1, 2), 3), ("V", piece(1, 3), 4)):
        key = "R%s%d" % (e, w)
        if e == "V":
            ts(T.Rr[:, a:b], T.land[:, a:b], float(SH), None, ALU.add, None, ["land%d" % w], [key])
        else:
            act(T.Rr[:, a:b], T.land[:, a:b], ACT.Identity, ["land%d" % w], [key], bias=float(SH))
        RR.append(key)
    dma("S", "dC", T.Rw[:, 0:W + 8], T.Rr[:], RR, ["R"])

    def table(t, i):
        if i % 2:
            return (T.lti[:], LT) if t == 0 else (T.Lw[:], LN)
        return (T.Rr[:], RR) if t == 0 else (T.Rw[:, 0:W + 8], ["R"])

    def offs(t, i):
        return (col("vo", t), "vo") if i == 0 else (col("xo", i), "xo%d" % i)

    def bank(i):
        return "PX%d" % (i % 2)

    def step(t, i):
        win, keys = table(t, i)
        o, ok = offs(t, i)
        m = ("mb%d" if i % 2 else "ma%d") % t
        tt(full("H%d" % i), win.indirect(o), full(m), ALU.mult, keys + [ok, m], ["H%d" % i])

    def spread(i, stop=True):
        b = bank(i + 1)
        terms = [(T.I16[:], T.KE[:], ["I16", "KE"])]
        for j in range(16):
            terms.append((T.B16[:, 15 - j:143 - j], T["H%d" % i][:, j:E:16], ["B16", "H%d" % i]))
        mm(b, T[b][:, 0:K], terms, stop=stop)

    def take(i):
        cp(col("xo", i), T[bank(i)][:, 0:K], [bank(i)], ["xo%d" % i])

    def ended(i, e="A"):
        b, bias = bank(i), "bL" if i % 2 else "bR"
        if e == "A":
            act(col("zz", i), T[b][:, 0:K], ACT.Identity, [b, bias], ["zz%d" % i], bias=T[bias][:], scale=1024.0)
        else:
            ts(col("zz", i), T[b][:, 0:K], 1024.0, T[bias][:], ALU.mult, ALU.add, [b, bias], ["zz%d" % i])

    def spare(i):
        tt(col("mx", i), T[bank(i)][:, 0:K], col("zz", i), ALU.max, [bank(i), "zz%d" % i], ["mx%d" % i])

    def spare2(i, n=1):
        cp(col("so", i, 0, n * K), col("mx", i, 0, n * K), ["mx%d" % j for j in range(i, i + n)],
           ["so%d" % j for j in range(i, i + n)])

    def column(t, i, e="A"):
        win, keys = table(t, i)
        o, ok = offs(t, i)
        if e == "A":
            act(full("G%d" % i), win.indirect(o), ACT.Identity, keys + [ok], ["G%d" % i])
        else:
            cp(full("G%d" % i), win.indirect(o), keys + [ok], ["G%d" % i])

    def out(i, b):
        act(full("N%d" % i), full(b), ACT.Identity, [b], ["N%d" % i], bias=-float(NL) if i == 1 else 0.0)

    def scatter_left(t, i, a=0, b=K):
        d = "DL%d" % t
        tt(T[d][:].indirect(col("so", i, a, b)), full("N%d" % i, a, b), full("sg%d" % t, a, b), ALU.mult,
           ["so%d" % i, "N%d" % i, "sg%d" % t], [d])

    def change_right(i, b):
        tt(full("E%d" % i), full(b), full("sg0"), ALU.mult, [b, "sg0"], ["E%d" % i])

    def new_right(i, b):
        lin(b, [("I16", "G%d" % i), ("I16", "E%d" % i)])

    def scatter_right(i):
        o, ok = (col("vo", 0), "vo") if i == 0 else (col("so", i), "so%d" % i)
        op("A", lambda: A.activation(T.Rw[:].indirect(o), full("N%d" % i), ACT.Silu), [ok, "N%d" % i], ["R"])

    def begin(b, m, x):
        lin(b, [(m, x)], stop=False)

    def end(b, *terms):
        lin(b, list(terms), start=False)

    def signs(t, b):
        lin(b, [("I2", "ma%d" % t), ("nI16", "mb%d" % t)])
        act(full("sg%d" % t), full(b), ACT.Sign, [b], ["sg%d" % t])

    step(0, 0)
    act(full("sv"), T.Rr[:].indirect(col("vo", 0)), ACT.Sign, RR + ["vo"], ["sv"], bias=0.5 - NL)
    act(full("Zu"), full("PC"), ACT.Relu, ["PC"], ["Zu"], bias=-BIG)
    lin("PB", [("Mb", "sv")]); spread(0)
    act(full("mb0"), full("PB"), ACT.Relu, ["PB", "bM"], ["mb0"], bias=T.bM[:], scale=0.5)
    scatter_u(0, 16, K)
    take(1); step(0, 1); ended(1); signs(0, "PC"); end("PA", ("nO16", "H0"), ("nI16", "Zu"))
    spare(1); change_right(0, "PA"); spread(1); lin("PB", [("I16", NV[0]), ("O16", "H1")]); column(0, 0)
    take(2); ended(2); new_right(0, "PC"); step(0, 2); out(1, "PB"); spare(2); spare2(1, 2)
    spread(2); lin("PA", [("O16", "H0"), ("nO16", "H2")]); scatter_left(0, 1, 0, 12)
    take(3); step(0, 3); begin("PB", "nO16", "H1"); out(0, "PC"); column(0, 2); scatter_right(0); scatter_left(0, 1, 12, 18)
    begin("PC", "I16", "G2"); change_right(2, "PA"); spread(3); ended(3); end("PB", ("O16", "H3"))
    take(4); begin("PA", "O16", "H2"); scatter_left(0, 1, 18, 22); end("PC", ("I16", "E2")); step(0, 4)
    ended(4); out(3, "PB"); spare(3); end("PA", ("nO16", "H4")); spare(4); out(2, "PC")
    scatter_left(0, 1, 22, K); spare2(3, 2); begin("PB", "O16", "KL"); change_right(4, "PA"); column(0, 4)
    scatter_left(0, 3); spread(4); scatter_right(2); new_right(4, "PC"); ended(5); end("PB", ("nO16", "H3"))
    spare(5); tt(full("N5"), full("PB"), full("sg0"), ALU.mult, ["PB", "sg0"], ["N5"]); out(4, "PC"); spare2(5); scatter_right(4)
    cp(T.DL0[:].indirect(col("so", 5)), full("N5"), ["so5", "N5"], ["DL0"])

    begin("PX0", "I16", NV[1])
    for k in range(3):
        hold(k, [("I16", "L16")])
    column(1, 0)
    tt(full("fu"), T.DL0[:, 0:NL].indirect(col("uo", 1)), full("Wu"), ALU.is_equal, ["DL0", "uo", "Wu"], ["fu"])
    ts(full("sv"), full("G0"), float(NL), None, ALU.is_equal, None, ["G0"], ["sv"])
    lin("PA", [("I16", "G0"), ("MB", "fu")])
    act(full("H0"), full("PA"), ACT.Relu, ["PA"], ["H0"], bias=-BIG)
    lin("PB", [("Mb", "sv")]); end("PX0", ("MB", "fu")); spread(0)
    act(full("mb1"), full("PB"), ACT.Relu, ["PB"], ["mb1"])
    act(full("Xu"), full("PX0"), ACT.Relu, ["PX0"], ["Xu"], bias=(NR - NL - BIG) * SH, scale=float(SH))
    merge(0, 0); merge(0, 2); merge(0, 1)
    for k in (0, 2, 1):
        narrow("L16", "Lw", k, "L%d" % k)
    ts(full("ma1"), full("H0"), 0.0, None, ALU.is_gt, None, ["H0"], ["ma1"])
    take(1); ended(1); begin("PA", "I16", NV[1]); step(1, 1); signs(1, "PC"); spare(1); spare2(1)
    spread(1); end("PA", ("O16", "H1")); out(1, "PA")
    take(2); step(1, 2); spread(2); scatter_left(1, 1, 0, 12); begin("PA", "nO16", "H1")
    op("A", lambda: A.activation(T.DU[:].indirect(col("uo", 1)), full("Xu"), ACT.Silu), ["uo", "Xu"], ["DU"])
    for k in (2, 0, 1):
        narrow("U16", "DU", k)
    take(3); step(1, 3); ended(3, "V"); hold(0, [("I16", "L16")], stop=False); hold(2, [("I16", "L16")], stop=False)
    spread(3); scatter_left(1, 1, 12, 24); spare(3); scatter_left(1, 1, 24, K); end("PA", ("O16", "H3")); out(3, "PA")
    take(4); lin("PB", [("nO16", "H3")]); spare2(3); step(1, 4); colours(1, "PC"); spread(4); ended(5)
    act(full("N5"), full("PB"), ACT.Identity, ["PB"], ["N5"], bias=float(NR))
    colours(0, "PC"); hold(1, [("I16", "L16")], stop=False)
    for k in (2, 0, 1):
        hold(k, [("IU", "U16")], start=False)
    scatter_left(1, 3, 0, 20); spare(5); scatter_left(1, 3, 20, K); spare2(5); scatter_left(1, 5)
    for j, k in enumerate((2, 0, 1)):
        a, b = BANKS[k]
        merge(1, k)
        dma("SA"[j % 2], "dO", T.yl[:, a:b], T.Lw[:, SH + a:SH + b], ["L%d" % k], [])
    wait("G", [(s, v) for s, v in count.items()])
